import numpy as np
import ml_dtypes


def mxq(x, axis, fmt="e4m3"):
    dtype, down = {"e4m3": (ml_dtypes.float8_e4m3fn, 7), "e5m2": (ml_dtypes.float8_e5m2, 14)}[fmt]
    v = np.moveaxis(np.asarray(x, np.float32).astype(ml_dtypes.bfloat16).astype(np.float64), axis, -1)
    blocks = v.reshape(v.shape[:-1] + (-1, 32))
    amax = np.abs(blocks).max(-1, keepdims=True)
    byte = np.maximum(np.where(amax > 0, np.frexp(amax)[1] - 1 + 127, 0) - down, 1)
    scale = np.exp2(byte - 127.0)
    codes = (blocks / scale).astype(np.float32).astype(dtype).astype(np.float64)
    return np.moveaxis((codes * scale).reshape(v.shape), -1, axis)


WIDE = False


def mx_kscale(k):
    if not WIDE:
        return np.ones(k)
    levels = np.array([10, -10, 5, -5, 0])
    if k % 512:
        return np.exp2(np.random.permutation(np.resize(levels, k // 32))).repeat(32)
    a = np.empty((k // 512, 16))
    for p in range(k // 512):
        a[p, :8] = np.random.permutation(np.resize(levels, 8))
        for g in range(8):
            far = levels[np.abs(levels - a[p, g]) >= 10]
            a[p, g + 8] = far[np.random.randint(len(far))]
    return np.exp2(a.ravel()).repeat(32)


def f64(x):
    return np.asarray(x).astype(np.float64)


def striped(idx):
    return np.tile(idx.reshape(-1, 16).T, (8, 1)).astype(np.uint16)


def unstriped(offs):
    return offs[:16].T.reshape(-1).astype(np.int64)


E2M1 = np.array([0.0, 0.5, 1.0, 1.5, 2.0, 3.0, 4.0, 6.0, -0.0, -0.5, -1.0, -1.5, -2.0, -3.0, -4.0, -6.0])


def pack_weight(w, fmt):
    k, n = w.shape
    w = f64(np.asarray(w, np.float32).astype(ml_dtypes.bfloat16)).reshape(k // 32, 32, n)
    amax = np.abs(w).max(1)
    if fmt == "e4m3":
        byte = np.frexp(amax)[1] - 1 + 127 - 7
    else:
        mant, ex = np.frexp(amax / 6.0)
        byte = np.where(mant > 0.5, ex, ex - 1) + 127
    byte = np.clip(np.where(amax > 0, byte, 1), 1, 254)
    scaled = (w * np.exp2(127.0 - byte)[:, None, :]).reshape(k, n).astype(np.float32)
    by_word = np.ascontiguousarray(scaled.reshape(k // 512, 128, 4, n).transpose(0, 1, 3, 2))
    if fmt == "e4m3":
        words = by_word.astype(ml_dtypes.float8_e4m3fn).view(np.uint8)
    else:
        c = by_word.astype(ml_dtypes.float4_e2m1fn).view(np.uint8) & 0xF
        words = (c[..., 0::2] | (c[..., 1::2] << 4)).reshape(k // 512, 128, 2 * n)
    return np.ascontiguousarray(words), np.ascontiguousarray(byte.astype(np.uint8).reshape(k // 512, 16, n))


def unpack_weight(words, scales, fmt):
    g, _, n = scales.shape
    words = np.ascontiguousarray(words).reshape(g, 128, n, -1)
    if fmt == "e4m3":
        vals = words.view(ml_dtypes.float8_e4m3fn).astype(np.float64)
    else:
        nib = np.empty((g, 128, n, 4), np.uint8)
        nib[..., 0::2] = words & 0xF
        nib[..., 1::2] = words >> 4
        vals = E2M1[nib]
    vals = vals * np.repeat(np.exp2(scales.astype(np.float64) - 127.0), 8, axis=1)[..., None]
    return vals.transpose(0, 1, 3, 2).reshape(g * 512, n)


def sigmoid(v):
    return 1.0 / (1.0 + np.exp(-np.maximum(v, -700.0)))


K, T, E, C, H, N = 512, 1280, 4, 256, 1024, 256


def by_expert(wq, xq):
    return np.concatenate([wq[e].T @ xq[:, e * C:(e + 1) * C] for e in range(E)], axis=1)


def setup_inputs():
    n = np.random.standard_normal
    s = mx_kscale(K)[:, None]
    u = mx_kscale(H)
    w1 = [pack_weight(m, "e2m1") for m in n((E, K, H)) / np.sqrt(K) / s[None]]
    w3 = [pack_weight(m, "e2m1") for m in n((E, K, H)) / np.sqrt(K) / s[None] * u[None, None, :]]
    w2 = [pack_weight(m, "e2m1") for m in n((E, H, N)) / np.sqrt(H) / u[None, :, None]]
    return {
        "xT": (n((K, T)) * s).astype(np.float32),
        "xr": n((N, T)).astype(np.float32),
        "w1_words": np.stack([m[0] for m in w1]),
        "w1_scales": np.stack([m[1] for m in w1]),
        "w3_words": np.stack([m[0] for m in w3]),
        "w3_scales": np.stack([m[1] for m in w3]),
        "w2_words": np.stack([m[0] for m in w2]),
        "w2_scales": np.stack([m[1] for m in w2]),
        "gate": np.tile(np.random.uniform(0.2, 1.0, E * C), (N, 1)).astype(np.float32),
        "offs": striped(np.random.permutation(T)[:E * C]),
    }


def reference(xT, xr, w1_words, w1_scales, w3_words, w3_scales, w2_words, w2_scales, gate, offs):
    idx = unstriped(offs)
    w1 = np.stack([unpack_weight(w1_words[e], w1_scales[e], "e2m1") for e in range(E)])
    w3 = np.stack([unpack_weight(w3_words[e], w3_scales[e], "e2m1") for e in range(E)])
    w2 = np.stack([unpack_weight(w2_words[e], w2_scales[e], "e2m1") for e in range(E)])
    xq = mxq(f64(xT)[:, idx], 0, "e4m3")
    h = sigmoid(by_expert(w1, xq))
    h = h * by_expert(w3, xq)
    y = by_expert(w2, mxq(h, 0, "e4m3"))
    out = f64(xr).copy()
    out[:, idx] += f64(gate) * y
    return out

@@ -1,0 +1,232 @@
+from contextlib import ExitStack
+
+import concourse.mybir as mybir
+from concourse.masks import make_identity
+
+K, T, E, C, H, N = 512, 1280, 4, 256, 1024, 256
+FLOPS = 2 * E * C * (2 * K * H + H * N)
+
+F32 = mybir.dt.float32
+BF16 = mybir.dt.bfloat16
+I32 = mybir.dt.int32
+U32 = mybir.dt.uint32
+U16 = mybir.dt.uint16
+U8 = mybir.dt.uint8
+FP8X4 = mybir.dt.float8_e4m3fn_x4
+FP4X4 = mybir.dt.float4_e2m1fn_x4
+SIGMOID = mybir.ActivationFunctionType.Sigmoid
+MULT = mybir.AluOpType.mult
+ADD = mybir.AluOpType.add
+
+P = 128
+PACK = 4
+LOADS = (512, 640, 128)
+CAST = 256
+SCALAR_SHARE = 8
+HALF = 512
+GATHERS = (0, 160, 512, 768, 1024)
+SCATTERS = (0, 256, 512, 704, 864, 1024)
+AFTER_PRODUCT = {
+    (1, 1, 1): ((0, 0),),
+    (2, 0, 1): ((0, 1),),
+    (2, 1, 1): ((1, 0),),
+    (3, 0, 1): ((1, 1),),
+    (3, 1, 1): ((2, 0), (2, 1)),
+}
+AFTER_TURN = {(3, 1): ((3, 0), (3, 1))}
+PIECES = (((0, 640), (640, 1280)), ((0, 512), (512, 1024), (1024, 1280)))
+
+
+def tile_moe_res_glu_sigmoid_kernel(
+    tc, xT, xr, w1_words, w1_scales, w3_words, w3_scales, w2_words, w2_scales, gate, offs, out
+):
+    nc = tc.nc
+    with ExitStack() as ctx:
+        keep = ctx.enter_context(tc.tile_pool(name="keep", bufs=1))
+        ring = ctx.enter_context(tc.tile_pool(name="ring", bufs=4))
+        psum = ctx.enter_context(tc.psum_pool(name="psum", bufs=1))
+
+        warm = keep.tile([P, 1], F32, name="warm")
+        nc.vector.memset(warm[:], 0.0)
+        warmed = keep.tile([P, 1], F32, name="warmed")
+        nc.scalar.activation(warmed[:], warm[:], SIGMOID)
+
+        first = keep.tile([P, 1, 2, H], U8, align_bytes=64, name="first")
+        first_i = first[:].rearrange("p e m i -> p (e m i)").bitcast(I32)
+        nc.vector.memset(first_i, 0)
+        first_i = first_i.rearrange("p (e m i) -> p e m i", e=1, m=2)
+        codes = keep.tile([P, T], U32, align_bytes=64, name="codes")
+        scales = keep.tile([P, T], U8, align_bytes=64, name="scales")
+        nc.gpsimd.memset(scales[:], 0)
+        rest = keep.tile([P, E - 1, 2, H], U8, align_bytes=64, name="rest")
+        rest_i = rest[:].rearrange("p e m i -> p (e m i)").bitcast(I32)
+        nc.vector.memset(rest_i, 0)
+        rest_i = rest_i.rearrange("p (e m i) -> p e m i", e=E - 1, m=2)
+        planes2 = keep.tile([P, E, 2, N], U8, align_bytes=64, name="planes2")
+        planes2_i = planes2[:].rearrange("p e s n -> p (e s n)").bitcast(I32)
+        nc.vector.memset(planes2_i, 0)
+        planes2_i = planes2_i.rearrange("p (e s n) -> p e s n", e=E, s=2)
+        windows = []
+        for r in range(N // P):
+            window = keep.tile([P, T], F32, name=f"window{r}")
+            (nc.gpsimd if r == 0 else nc.vector).memset(window[:], 0.0)
+            windows.append(window)
+        ident = keep.tile([P, P], F32, name="ident")
+        make_identity(nc, ident[:])
+
+        words0 = keep.tile([P, 2, 2 * H], U8, align_bytes=64, name="words0")
+        words0_i = words0[:].rearrange("p m b -> p (m b)").bitcast(I32).rearrange("p (m b) -> p m b", m=2)
+        later = keep.tile([P, E - 1, 2, 2 * H], U8, align_bytes=64, name="later")
+        later_i = later[:].rearrange("p e m b -> p (e m b)").bitcast(I32).rearrange("p (x b) -> p x b", b=H // 2)
+        words2 = keep.tile([P, E, 2, 2 * N], U8, align_bytes=64, name="words2")
+        words2_i = words2[:].rearrange("p e s b -> p (e s b)").bitcast(I32).rearrange("p (x b) -> p x b", b=N // 2)
+        gates = keep.tile([P, N // P, E * C], F32, name="gates")
+        residual = keep.tile([P, N // P, T], F32, name="residual")
+        nc.gpsimd.memset(later_i[:, :, 0:1], 0)
+        nc.gpsimd.memset(words2_i[:, :, 0:1], 0)
+        nc.gpsimd.memset(gates[:, 0, 0:1], 0.0)
+        nc.gpsimd.memset(residual[:, 0, 0:1], 0.0)
+
+        s1_i, s3_i, s2_i = w1_scales.bitcast(I32), w3_scales.bitcast(I32), w2_scales.bitcast(I32)
+        w1_i, w3_i, w2_i = w1_words.bitcast(I32), w3_words.bitcast(I32), w2_words.bitcast(I32)
+        raws = []
+        t0 = 0
+        for c, width in enumerate(LOADS):
+            raw = keep.tile([P, PACK, width], F32, name=f"raw{c}")
+            nc.sync.dma_start(raw[:], xT.rearrange("(p j) t -> p j t", j=PACK)[:, :, t0 : t0 + width])
+            raws.append((t0, width, raw))
+            t0 += width
+            if c == 0:
+                offsets = keep.tile([P, E * C // 16], U16, name="offsets")
+                nc.sync.dma_start(offsets[:], offs)
+        for r in range(4):
+            for m, src in enumerate((s1_i, s3_i)):
+                nc.sync.dma_start(first_i[r:P:32, 0, m, :], src[0, 0, r:16:4, :])
+        for s in range(2):
+            part = slice(s * HALF // 2, (s + 1) * HALF // 2)
+            for m, src in enumerate((w1_i, w3_i)):
+                nc.sync.dma_start(words0_i[:, m, part], src[0, 0][:, part])
+        nc.sync.dma_start(words2_i[:, 0:2, :], w2_i[0].rearrange("s p b -> p s b"))
+        for r in range(4):
+            nc.sync.dma_start(
+                planes2_i[r:P:32].rearrange("q e s n -> q (e s) n"),
+                s2_i[:, :, r:16:4, :].rearrange("e s q n -> q (e s) n"),
+            )
+        for r in range(4):
+            for m, src in enumerate((s1_i, s3_i)):
+                nc.sync.dma_start(rest_i[r:P:32, :, m, :], src[1:E, 0, r:16:4, :].rearrange("e q i -> q e i"))
+        for e in range(1, E):
+            for m, src in enumerate((w1_i, w3_i)):
+                nc.sync.dma_start(later_i[:, 2 * (e - 1) + m, :], src[e, 0])
+            nc.sync.dma_start(words2_i[:, 2 * e : 2 * e + 2, :], w2_i[e].rearrange("s p b -> p s b"))
+            if e == 1:
+                nc.sync.dma_start(gates[:], gate.rearrange("(r p) j -> p r j", p=P))
+        nc.sync.dma_start(residual[:], xr.rearrange("(r p) t -> p r t", p=P))
+
+        grouped = keep.tile([P, T, PACK], BF16, align_bytes=64, name="grouped")
+        for t0, width, raw in raws:
+            for c in range(0, width, CAST):
+                end = min(c + CAST, width)
+                cut = c + 3 * (end - c) // SCALAR_SHARE
+                for copy, a, b in ((nc.scalar.copy, c, cut), (nc.vector.tensor_copy, cut, end)):
+                    copy(
+                        grouped[:, t0 + a : t0 + b, :].rearrange("p (c i) j -> p c j i", i=4),
+                        raw[:, :, a:b].rearrange("p j (c i) -> p c j i", i=4),
+                    )
+                cols = slice(t0 + c, t0 + end)
+                nc.vector.quantize_mx(
+                    out=codes[:, cols].bitcast(FP8X4),
+                    scales=scales[:, cols],
+                    in_=grouped[:, cols, :].rearrange("p t j -> p (t j)"),
+                )
+
+        x_codes = keep.tile([P, E * C], U32, align_bytes=64, name="x_codes")
+        x_scales = keep.tile([P, E * C], U8, align_bytes=64, name="x_scales")
+        y = keep.tile([P, N // P, E * C], F32, name="y")
+
+        def gather(g):
+            part = slice(GATHERS[g], GATHERS[g + 1])
+            entries = offsets[:, part.start // 16 : part.stop // 16]
+            nc.vector.tensor_copy(x_codes[:, part], codes[:].indirect(entries))
+            nc.vector.tensor_copy(x_scales[:, part], scales[:].indirect(entries))
+
+        def scatter(g, r):
+            part = slice(SCATTERS[g], SCATTERS[g + 1])
+            entries = offsets[:, part.start // 16 : part.stop // 16]
+            nc.vector.tensor_tensor(windows[r][:].indirect(entries), y[:, r, part], gates[:, r, part], MULT)
+
+        token = keep.tile([P, 10], F32, name="token")
+
+        def scatter_after(event, later):
+            for g, r in later:
+                nc.gpsimd.tensor_tensor(token[:, 2 * g + r : 2 * g + r + 1], windows[r][:, 0:1], event, ADD)
+                scatter(g, r)
+
+        gather(0)
+        gather(1)
+        for e in range(E):
+            for q in range(C // P):
+                slots = slice(e * C + q * P, e * C + (q + 1) * P)
+                h = ring.tile([P, H], BF16, align_bytes=64, name="h")
+                for s in range(H // HALF):
+                    i_cols = slice(s * HALF, (s + 1) * HALF)
+                    banks = []
+                    for m in range(2):
+                        words = words0[:, m, :] if e == 0 else later[:, e - 1, m, :]
+                        plane = first[:, 0, m, i_cols] if e == 0 else rest[:, e - 1, m, i_cols]
+                        bank = psum.tile([P, HALF], F32, name=f"bank{m}", bufs=3)
+                        nc.tensor.matmul_mx(
+                            out=bank[:],
+                            lhsT=x_codes[:, slots].bitcast(FP8X4),
+                            lhsT_scale=x_scales[:, slots],
+                            rhs=words[:, 2 * s * HALF : 2 * (s + 1) * HALF].bitcast(FP4X4),
+                            rhs_scale=plane,
+                            start=True,
+                            stop=True,
+                        )
+                        banks.append(bank[:].rearrange("p (w u k) -> p u w k", u=2, k=2))
+                    sig = ring.tile([P, HALF], F32, name="sig")
+                    sig_v = sig[:].rearrange("p (u w k) -> p u w k", u=2, k=2)
+                    nc.scalar.activation(sig_v, banks[0], SIGMOID)
+                    nc.vector.tensor_tensor(
+                        h[:, i_cols].rearrange("p (u w k) -> p u w k", u=2, k=2), banks[1], sig_v, MULT
+                    )
+                    if e == 0 and q == 1:
+                        gather(2 + s)
+                    scatter_after(h[:, s * HALF : s * HALF + 1], AFTER_PRODUCT.get((e, q, s), ()))
+                turned = psum.tile([P, 2, 2, P], F32, name="turned")
+                for s in range(2):
+                    for u in range(2):
+                        b = 2 * s + u
+                        nc.tensor.transpose(turned[:, s, u, :], h[:].bitcast(F32)[:, b * P : (b + 1) * P], ident[:])
+                hg = ring.tile([P, 2, P, PACK], BF16, align_bytes=64, name="hg")
+                nc.scalar.copy(
+                    hg[:].rearrange("p s c k -> p (s c k)").bitcast(F32).rearrange("p (s c u) -> p s c u", s=2, u=2),
+                    turned[:].rearrange("p s u c -> p s c u"),
+                )
+                scatter_after(hg[:, 0, 0, 0:1], AFTER_TURN.get((e, q), ()))
+                h_codes = ring.tile([P, 2 * P], U32, align_bytes=64, name="h_codes")
+                h_scales = ring.tile([P, 2 * P], U8, align_bytes=64, name="h_scales")
+                nc.vector.quantize_mx(
+                    out=h_codes[:].bitcast(FP8X4), scales=h_scales[:], in_=hg[:].rearrange("p s c k -> p (s c k)")
+                )
+                y_bank = psum.tile([P, N // P, P], F32, name="y_bank")
+                for r in range(N // P):
+                    for s in range(2):
+                        nc.tensor.matmul_mx(
+                            out=y_bank[:, r, :],
+                            lhsT=words2[:, e, s, 2 * r * P : 2 * (r + 1) * P].bitcast(FP4X4),
+                            lhsT_scale=planes2[:, e, s, r * P : (r + 1) * P],
+                            rhs=h_codes[:, s * P : (s + 1) * P].bitcast(FP8X4),
+                            rhs_scale=h_scales[:, s * P : (s + 1) * P],
+                            start=(s == 0),
+                            stop=(s == 1),
+                        )
+                nc.scalar.copy(y[:, :, slots], y_bank[:])
+        for r in range(N // P):
+            scatter(4, r)
+            total = keep.tile([P, T], F32, name=f"total{r}")
+            for a, b in PIECES[r]:
+                piece = slice(a, b)
+                nc.vector.tensor_tensor(total[:, piece], windows[r][:, piece], residual[:, r, piece], ADD)
+                nc.sync.dma_start(out[r * P : (r + 1) * P, piece], total[:, piece])

@@ -20,20 +20,15 @@ ADD = mybir.AluOpType.add
 
 P = 128
 PACK = 4
-LOADS = (512, 640, 128)
+LOADS = (512, 384, 256, 128)
 CAST = 256
 SCALAR_SHARE = 8
 HALF = 512
-GATHERS = (0, 160, 512, 768, 1024)
-SCATTERS = (0, 256, 512, 704, 864, 1024)
-AFTER_PRODUCT = {
-    (1, 1, 1): ((0, 0),),
-    (2, 0, 1): ((0, 1),),
-    (2, 1, 1): ((1, 0),),
-    (3, 0, 1): ((1, 1),),
-    (3, 1, 1): ((2, 0), (2, 1)),
-}
-AFTER_TURN = {(3, 1): ((3, 0), (3, 1))}
+FIRST = 160
+LAG = 3
+EARLY = 1
+AHEAD = 3
+SPARE = 512
 PIECES = (((0, 640), (640, 1280)), ((0, 512), (512, 1024), (1024, 1280)))
 
 
@@ -46,84 +41,67 @@ def tile_moe_res_glu_sigmoid_kernel(
         ring = ctx.enter_context(tc.tile_pool(name="ring", bufs=4))
         psum = ctx.enter_context(tc.psum_pool(name="psum", bufs=1))
 
-        warm = keep.tile([P, 1], F32, name="warm")
-        nc.vector.memset(warm[:], 0.0)
-        warmed = keep.tile([P, 1], F32, name="warmed")
+        first = keep.tile([P, EARLY, 2, H], U8, align_bytes=64, name="first")
+        first_i = first[:].rearrange("p e m i -> p (e m i)").bitcast(I32)
+        nc.gpsimd.memset(first_i, 0)
+        first_i = first_i.rearrange("p (e m i) -> p e m i", e=EARLY, m=2)
+        warm = keep.tile([P, 1], F32, align_bytes=64, name="warm", tag="stage1")
+        nc.gpsimd.memset(warm[:], 0.0)
+        zero = keep.tile([P, 1], F32, name="zero")
+        nc.gpsimd.memset(zero[:], 0.0)
+        warmed = keep.tile([P, 1], F32, align_bytes=64, name="warmed", tag="words0")
         nc.scalar.activation(warmed[:], warm[:], SIGMOID)
 
-        first = keep.tile([P, 1, 2, H], U8, align_bytes=64, name="first")
-        first_i = first[:].rearrange("p e m i -> p (e m i)").bitcast(I32)
-        nc.vector.memset(first_i, 0)
-        first_i = first_i.rearrange("p (e m i) -> p e m i", e=1, m=2)
         codes = keep.tile([P, T], U32, align_bytes=64, name="codes")
         scales = keep.tile([P, T], U8, align_bytes=64, name="scales")
-        nc.gpsimd.memset(scales[:], 0)
-        rest = keep.tile([P, E - 1, 2, H], U8, align_bytes=64, name="rest")
+        nc.vector.memset(scales[:].bitcast(I32), 0)
+        rest = keep.tile([P, E - EARLY, 2, H], U8, align_bytes=64, name="rest")
         rest_i = rest[:].rearrange("p e m i -> p (e m i)").bitcast(I32)
         nc.vector.memset(rest_i, 0)
-        rest_i = rest_i.rearrange("p (e m i) -> p e m i", e=E - 1, m=2)
+        rest_i = rest_i.rearrange("p (e m i) -> p e m i", e=E - EARLY, m=2)
         planes2 = keep.tile([P, E, 2, N], U8, align_bytes=64, name="planes2")
         planes2_i = planes2[:].rearrange("p e s n -> p (e s n)").bitcast(I32)
         nc.vector.memset(planes2_i, 0)
         planes2_i = planes2_i.rearrange("p (e s n) -> p e s n", e=E, s=2)
         windows = []
         for r in range(N // P):
-            window = keep.tile([P, T], F32, name=f"window{r}")
-            (nc.gpsimd if r == 0 else nc.vector).memset(window[:], 0.0)
+            window = keep.tile([P, T + SPARE], F32, align_bytes=64, name=f"window{r}")
+            nc.scalar.copy(window[:, 0:T], zero[:].to_broadcast([P, T]))
             windows.append(window)
         ident = keep.tile([P, P], F32, name="ident")
         make_identity(nc, ident[:])
 
-        words0 = keep.tile([P, 2, 2 * H], U8, align_bytes=64, name="words0")
-        words0_i = words0[:].rearrange("p m b -> p (m b)").bitcast(I32).rearrange("p (m b) -> p m b", m=2)
-        later = keep.tile([P, E - 1, 2, 2 * H], U8, align_bytes=64, name="later")
-        later_i = later[:].rearrange("p e m b -> p (e m b)").bitcast(I32).rearrange("p (x b) -> p x b", b=H // 2)
-        words2 = keep.tile([P, E, 2, 2 * N], U8, align_bytes=64, name="words2")
-        words2_i = words2[:].rearrange("p e s b -> p (e s b)").bitcast(I32).rearrange("p (x b) -> p x b", b=N // 2)
-        gates = keep.tile([P, N // P, E * C], F32, name="gates")
-        residual = keep.tile([P, N // P, T], F32, name="residual")
-        nc.gpsimd.memset(later_i[:, :, 0:1], 0)
-        nc.gpsimd.memset(words2_i[:, :, 0:1], 0)
-        nc.gpsimd.memset(gates[:, 0, 0:1], 0.0)
-        nc.gpsimd.memset(residual[:, 0, 0:1], 0.0)
-
         s1_i, s3_i, s2_i = w1_scales.bitcast(I32), w3_scales.bitcast(I32), w2_scales.bitcast(I32)
         w1_i, w3_i, w2_i = w1_words.bitcast(I32), w3_words.bitcast(I32), w2_words.bitcast(I32)
-        raws = []
-        t0 = 0
-        for c, width in enumerate(LOADS):
-            raw = keep.tile([P, PACK, width], F32, name=f"raw{c}")
-            nc.sync.dma_start(raw[:], xT.rearrange("(p j) t -> p j t", j=PACK)[:, :, t0 : t0 + width])
+        x_rows = xT.rearrange("(p j) t -> p j t", j=PACK)
+        offsets = keep.tile([P, E * C // 16], U16, name="offsets")
+        nc.sync.dma_start(offsets[:], offs)
+        raw0 = keep.tile([P, PACK, LOADS[0]], F32, align_bytes=64, name="raw0", tag="stage0")
+        nc.sync.dma_start(raw0[:], x_rows[:, :, 0 : LOADS[0]])
+        raws = [(0, LOADS[0], raw0[:])]
+        scale_loads = [
+            (first_i[r:P:32, :, m, :], rows[0:EARLY, 0, r:16:4, :].rearrange("e q i -> q e i"))
+            for m, rows in enumerate((s1_i, s3_i))
+            for r in range(4)
+        ]
+        for dst, src in scale_loads[:6]:
+            nc.sync.dma_start(dst, src)
+        raw1 = keep.tile([P, PACK * (T - LOADS[0])], F32, align_bytes=64, name="raw1", tag="stage1")
+        t0 = LOADS[0]
+        for width in LOADS[1:]:
+            at = PACK * (t0 - LOADS[0])
+            raw = raw1[:, at : at + PACK * width].rearrange("p (j t) -> p j t", j=PACK)
+            nc.sync.dma_start(raw, x_rows[:, :, t0 : t0 + width])
             raws.append((t0, width, raw))
             t0 += width
-            if c == 0:
-                offsets = keep.tile([P, E * C // 16], U16, name="offsets")
-                nc.sync.dma_start(offsets[:], offs)
-        for r in range(4):
-            for m, src in enumerate((s1_i, s3_i)):
-                nc.sync.dma_start(first_i[r:P:32, 0, m, :], src[0, 0, r:16:4, :])
-        for s in range(2):
-            part = slice(s * HALF // 2, (s + 1) * HALF // 2)
-            for m, src in enumerate((w1_i, w3_i)):
-                nc.sync.dma_start(words0_i[:, m, part], src[0, 0][:, part])
-        nc.sync.dma_start(words2_i[:, 0:2, :], w2_i[0].rearrange("s p b -> p s b"))
-        for r in range(4):
-            nc.sync.dma_start(
-                planes2_i[r:P:32].rearrange("q e s n -> q (e s) n"),
-                s2_i[:, :, r:16:4, :].rearrange("e s q n -> q (e s) n"),
-            )
-        for r in range(4):
-            for m, src in enumerate((s1_i, s3_i)):
-                nc.sync.dma_start(rest_i[r:P:32, :, m, :], src[1:E, 0, r:16:4, :].rearrange("e q i -> q e i"))
-        for e in range(1, E):
-            for m, src in enumerate((w1_i, w3_i)):
-                nc.sync.dma_start(later_i[:, 2 * (e - 1) + m, :], src[e, 0])
-            nc.sync.dma_start(words2_i[:, 2 * e : 2 * e + 2, :], w2_i[e].rearrange("s p b -> p s b"))
-            if e == 1:
-                nc.sync.dma_start(gates[:], gate.rearrange("(r p) j -> p r j", p=P))
-        nc.sync.dma_start(residual[:], xr.rearrange("(r p) t -> p r t", p=P))
+        for dst, src in scale_loads[6:]:
+            nc.sync.dma_start(dst, src)
+        words0 = keep.tile([P, 2 * 2 * H], U8, align_bytes=64, name="words0", tag="words0")
+        words0_i = words0[:].bitcast(I32).rearrange("p (m b) -> p m b", m=2)
+        for m, src in enumerate((w1_i, w3_i)):
+            nc.sync.dma_start(words0_i[:, m, :], src[0, 0])
 
-        grouped = keep.tile([P, T, PACK], BF16, align_bytes=64, name="grouped")
+        grouped = keep.tile([P, T, PACK], BF16, align_bytes=64, name="grouped", tag="grouped")
         for t0, width, raw in raws:
             for c in range(0, width, CAST):
                 end = min(c + CAST, width)
@@ -140,91 +118,155 @@ def tile_moe_res_glu_sigmoid_kernel(
                     in_=grouped[:, cols, :].rearrange("p t j -> p (t j)"),
                 )
 
-        x_codes = keep.tile([P, E * C], U32, align_bytes=64, name="x_codes")
-        x_scales = keep.tile([P, E * C], U8, align_bytes=64, name="x_scales")
-        y = keep.tile([P, N // P, E * C], F32, name="y")
+        later = keep.tile([P, 2 * (E - 1) * 2 * H], U8, align_bytes=64, name="later", tag="stage1")
+        later_i = later[:].bitcast(I32).rearrange("p (m e b) -> p m e b", m=2, e=E - 1)
+        words2 = keep.tile([P, E * 2 * 2 * N], U8, align_bytes=64, name="words2", tag="stage0")
+        words2_i = words2[:].bitcast(I32).rearrange("p (x b) -> p x b", b=N // 2)
+        gates = keep.tile([P, E * C], F32, align_bytes=64, name="gates", tag="grouped")[:]
+        for r in range(4):
+            nc.sync.dma_start(
+                planes2_i[r:P:32].rearrange("q e s n -> q (e s) n"),
+                s2_i[:, :, r:16:4, :].rearrange("e s q n -> q (e s) n"),
+            )
+        nc.sync.dma_start(words2_i[:, 0:E, :], w2_i[0 : E // 2].rearrange("e s p b -> p (e s) b"))
+        for r in range(4):
+            if r == 3:
+                for m, src in enumerate((w1_i, w3_i)):
+                    nc.sync.dma_start(later_i[:, m], src[1:E, 0].rearrange("e p b -> p e b"))
+            for m, src in ((1, s3_i), (0, s1_i)):
+                nc.sync.dma_start(rest_i[r:P:32, :, m, :], src[EARLY:E, 0, r:16:4, :].rearrange("e q i -> q e i"))
+        nc.sync.dma_start(gates, gate[0:P, :])
+        nc.sync.dma_start(words2_i[:, E:, :], w2_i[E // 2 : E].rearrange("e s p b -> p (e s) b"))
 
-        def gather(g):
-            part = slice(GATHERS[g], GATHERS[g + 1])
-            entries = offsets[:, part.start // 16 : part.stop // 16]
-            nc.vector.tensor_copy(x_codes[:, part], codes[:].indirect(entries))
-            nc.vector.tensor_copy(x_scales[:, part], scales[:].indirect(entries))
+        y = keep.tile([P, E, N // P, C], F32, name="y")
 
-        def scatter(g, r):
-            part = slice(SCATTERS[g], SCATTERS[g + 1])
-            entries = offsets[:, part.start // 16 : part.stop // 16]
-            nc.vector.tensor_tensor(windows[r][:].indirect(entries), y[:, r, part], gates[:, r, part], MULT)
+        def entries(a, b):
+            return offsets[:, a // 16 : b // 16]
 
-        token = keep.tile([P, 10], F32, name="token")
+        def scatter(e, r):
+            nc.vector.tensor_tensor(
+                windows[r][:].indirect(entries(e * C, (e + 1) * C)), y[:, e, r, :], gates[:, e * C : (e + 1) * C], MULT
+            )
 
-        def scatter_after(event, later):
-            for g, r in later:
-                nc.gpsimd.tensor_tensor(token[:, 2 * g + r : 2 * g + r + 1], windows[r][:, 0:1], event, ADD)
-                scatter(g, r)
+        head_codes = keep.tile([P, 2 * C], U32, align_bytes=64, name="head_codes")
+        head_scales = keep.tile([P, 2 * C], U8, align_bytes=64, name="head_scales")
+        for a, b in ((0, FIRST), (FIRST, 2 * C)):
+            nc.vector.tensor_copy(head_codes[:, a:b], codes[:].indirect(entries(a, b)))
+            nc.vector.tensor_copy(head_scales[:, a:b], scales[:].indirect(entries(a, b)))
+        x_codes = [head_codes[:, 0:C], head_codes[:, C : 2 * C]]
+        x_scales = [head_scales[:, 0:C], head_scales[:, C : 2 * C]]
 
-        gather(0)
-        gather(1)
-        for e in range(E):
-            for q in range(C // P):
-                slots = slice(e * C + q * P, e * C + (q + 1) * P)
-                h = ring.tile([P, H], BF16, align_bytes=64, name="h")
-                for s in range(H // HALF):
-                    i_cols = slice(s * HALF, (s + 1) * HALF)
-                    banks = []
-                    for m in range(2):
-                        words = words0[:, m, :] if e == 0 else later[:, e - 1, m, :]
-                        plane = first[:, 0, m, i_cols] if e == 0 else rest[:, e - 1, m, i_cols]
-                        bank = psum.tile([P, HALF], F32, name=f"bank{m}", bufs=3)
-                        nc.tensor.matmul_mx(
-                            out=bank[:],
-                            lhsT=x_codes[:, slots].bitcast(FP8X4),
-                            lhsT_scale=x_scales[:, slots],
-                            rhs=words[:, 2 * s * HALF : 2 * (s + 1) * HALF].bitcast(FP4X4),
-                            rhs_scale=plane,
-                            start=True,
-                            stop=True,
-                        )
-                        banks.append(bank[:].rearrange("p (w u k) -> p u w k", u=2, k=2))
-                    sig = ring.tile([P, HALF], F32, name="sig")
-                    sig_v = sig[:].rearrange("p (u w k) -> p u w k", u=2, k=2)
-                    nc.scalar.activation(sig_v, banks[0], SIGMOID)
-                    nc.vector.tensor_tensor(
-                        h[:, i_cols].rearrange("p (u w k) -> p u w k", u=2, k=2), banks[1], sig_v, MULT
-                    )
-                    if e == 0 and q == 1:
-                        gather(2 + s)
-                    scatter_after(h[:, s * HALF : s * HALF + 1], AFTER_PRODUCT.get((e, q, s), ()))
-                turned = psum.tile([P, 2, 2, P], F32, name="turned")
+        LATE = ((codes, x_codes, U32, 2, 3), (scales, x_scales, U8, 2, 4), (codes, x_codes, U32, 3, 4))
+        blocks = E * C // P
+        steps = blocks * H // HALF
+        banks = [(0, 1), (2, 3), (0, 4), (1, 5)]
+        for n in range(len(banks), steps):
+            banks.append(banks[n - AHEAD][::-1])
+        ready, hs, turned_h, y_banks = {}, {}, {}, {}
+
+        def first_products(n):
+            k, s = divmod(n, 2)
+            e, q = divmod(k, C // P)
+            slots = slice(q * P, (q + 1) * P)
+            i_cols = slice(s * HALF, (s + 1) * HALF)
+            pair = []
+            for m in range(2):
+                bank = psum.tile([P, HALF], F32, name="bank", tag=f"bank{banks[n][m]}")
+                pair.append(bank[:].rearrange("p (w u k) -> p u w k", u=2, k=2))
+                table, at = (words0, m) if e == 0 else (later, m * (E - 1) + e - 1)
+                at = 2 * (at * H + s * HALF)
+                plane = first[:, e, m, i_cols] if e < EARLY else rest[:, e - EARLY, m, i_cols]
+                nc.tensor.matmul_mx(
+                    out=bank[:],
+                    lhsT=x_codes[e][:, slots].bitcast(FP8X4),
+                    lhsT_scale=x_scales[e][:, slots],
+                    rhs=table[:, at : at + 2 * HALF].bitcast(FP4X4),
+                    rhs_scale=plane,
+                    start=True,
+                    stop=True,
+                )
+            if k < LAG and s == 1:
+                sig = keep.tile([P, HALF], F32, align_bytes=64, name="sig_once", tag=f"late{k}")[:]
+            elif s == 1:
+                sig = windows[(k - LAG) % 2][:, T : T + HALF]
+            else:
+                sig = keep.tile([P, HALF], F32, align_bytes=64, name="sig", tag=f"even{k % 2}")[:]
+            sig_v = sig.rearrange("p (u w k) -> p u w k", u=2, k=2)
+            nc.scalar.activation(sig_v, pair[0], SIGMOID)
+            ready[n] = (pair[1], sig_v)
+
+        def turn(k):
+            tag = f"bank{banks[2 * k + 2][0]}" if 2 * k + 2 < steps else "turned"
+            turned = psum.tile([P, 2, 2, P], F32, name="turned", tag=tag)
+            for s in range(2):
+                for u in range(2):
+                    b = 2 * s + u
+                    nc.tensor.transpose(turned[:, s, u, :], hs[k][:].bitcast(F32)[:, b * P : (b + 1) * P], ident[:])
+            if k == blocks - 1:
+                hg = windows[1][:, T : T + HALF]
+            else:
+                hg = ring.tile([P, HALF], F32, align_bytes=64, name="hg")[:]
+            nc.scalar.copy(
+                hg.rearrange("p (s c u) -> p s c u", s=2, u=2), turned[:].rearrange("p s u c -> p s c u")
+            )
+            turned_h[k] = hg
+
+        def quantise(k):
+            h_codes = keep.tile([P, 2 * P], U32, align_bytes=64, name="h_codes", tag=f"even{(k + 1) % 2}")
+            h_scales = ring.tile([P, 2 * P], U8, align_bytes=64, name="h_scales")
+            nc.vector.quantize_mx(out=h_codes[:].bitcast(FP8X4), scales=h_scales[:], in_=turned_h[k].bitcast(BF16))
+            return h_codes, h_scales
+
+        def second_product(k, h_codes, h_scales):
+            e, q = divmod(k, C // P)
+            if q == 0:
+                y_banks[e] = psum.tile([P, N // P, C], F32, name="y_bank")
+            for r in range(N // P):
                 for s in range(2):
-                    for u in range(2):
-                        b = 2 * s + u
-                        nc.tensor.transpose(turned[:, s, u, :], h[:].bitcast(F32)[:, b * P : (b + 1) * P], ident[:])
-                hg = ring.tile([P, 2, P, PACK], BF16, align_bytes=64, name="hg")
-                nc.scalar.copy(
-                    hg[:].rearrange("p s c k -> p (s c k)").bitcast(F32).rearrange("p (s c u) -> p s c u", s=2, u=2),
-                    turned[:].rearrange("p s u c -> p s c u"),
-                )
-                scatter_after(hg[:, 0, 0, 0:1], AFTER_TURN.get((e, q), ()))
-                h_codes = ring.tile([P, 2 * P], U32, align_bytes=64, name="h_codes")
-                h_scales = ring.tile([P, 2 * P], U8, align_bytes=64, name="h_scales")
-                nc.vector.quantize_mx(
-                    out=h_codes[:].bitcast(FP8X4), scales=h_scales[:], in_=hg[:].rearrange("p s c k -> p (s c k)")
-                )
-                y_bank = psum.tile([P, N // P, P], F32, name="y_bank")
-                for r in range(N // P):
-                    for s in range(2):
-                        nc.tensor.matmul_mx(
-                            out=y_bank[:, r, :],
-                            lhsT=words2[:, e, s, 2 * r * P : 2 * (r + 1) * P].bitcast(FP4X4),
-                            lhsT_scale=planes2[:, e, s, r * P : (r + 1) * P],
-                            rhs=h_codes[:, s * P : (s + 1) * P].bitcast(FP8X4),
-                            rhs_scale=h_scales[:, s * P : (s + 1) * P],
-                            start=(s == 0),
-                            stop=(s == 1),
-                        )
-                nc.scalar.copy(y[:, :, slots], y_bank[:])
+                    at = 2 * ((2 * e + s) * N + r * P)
+                    nc.tensor.matmul_mx(
+                        out=y_banks[e][:, r, q * P : (q + 1) * P],
+                        lhsT=words2[:, at : at + 2 * P].bitcast(FP4X4),
+                        lhsT_scale=planes2[:, e, s, r * P : (r + 1) * P],
+                        rhs=h_codes[:, s * P : (s + 1) * P].bitcast(FP8X4),
+                        rhs_scale=h_scales[:, s * P : (s + 1) * P],
+                        start=(s == 0),
+                        stop=(s == 1),
+                    )
+            if q == 1:
+                nc.scalar.copy(y[:, e], y_banks[e][:])
+
+        for n in range(AHEAD):
+            first_products(n)
+        for n in range(steps):
+            k, s = divmod(n, 2)
+            if s == 0:
+                hs[k] = ring.tile([P, H], BF16, align_bytes=64, name="h")
+            bank, sig_v = ready[n]
+            nc.vector.tensor_tensor(
+                hs[k][:, s * HALF : (s + 1) * HALF].rearrange("p (u w k) -> p u w k", u=2, k=2), bank, sig_v, MULT
+            )
+            if k < LAG and s == 1:
+                table, kept, dtype, a, b = LATE[k]
+                late = keep.tile([P, (b - a) * C], dtype, align_bytes=64, name="late", tag=f"late{k}")
+                nc.vector.tensor_copy(late[:], table[:].indirect(entries(a * C, b * C)))
+                kept.extend(late[:, c * C : (c + 1) * C] for c in range(b - a))
+            if s == 1:
+                if k >= LAG:
+                    scatter(*divmod(k - LAG, 2))
+                turn(k)
+            if s == 0 and k > 0:
+                quantised = quantise(k - 1)
+            if n + AHEAD < steps:
+                first_products(n + AHEAD)
+            if s == 0 and k > 0:
+                second_product(k - 1, *quantised)
+        second_product(blocks - 1, *quantise(blocks - 1))
+        residual = keep.tile([P, N // P, T], F32, align_bytes=64, name="residual", tag="words0")
+        nc.sync.dma_start(residual[:], xr.rearrange("(r p) t -> p r t", p=P))
+        scatter(E - 2, 1)
         for r in range(N // P):
-            scatter(4, r)
+            scatter(E - 1, r)
             total = keep.tile([P, T], F32, name=f"total{r}")
             for a, b in PIECES[r]:
                 piece = slice(a, b)

@@ -29,7 +29,8 @@ LAG = 3
 EARLY = 1
 AHEAD = 3
 SPARE = 512
-PIECES = (((0, 640), (640, 1280)), ((0, 512), (512, 1024), (1024, 1280)))
+TURNED = 6
+PIECES = ((0, 768, 1280), (1, 0, 512), (1, 512, 1024), (1, 1024, 1280))
 
 
 def tile_moe_res_glu_sigmoid_kernel(
@@ -47,10 +48,8 @@ def tile_moe_res_glu_sigmoid_kernel(
         first_i = first_i.rearrange("p (e m i) -> p e m i", e=EARLY, m=2)
         warm = keep.tile([P, 1], F32, align_bytes=64, name="warm", tag="stage1")
         nc.gpsimd.memset(warm[:], 0.0)
-        zero = keep.tile([P, 1], F32, name="zero")
-        nc.gpsimd.memset(zero[:], 0.0)
-        warmed = keep.tile([P, 1], F32, align_bytes=64, name="warmed", tag="words0")
-        nc.scalar.activation(warmed[:], warm[:], SIGMOID)
+        zero = keep.tile([P, 1], F32, align_bytes=64, name="zero", tag="words0")
+        nc.scalar.copy(zero[:], warm[:])
 
         codes = keep.tile([P, T], U32, align_bytes=64, name="codes")
         scales = keep.tile([P, T], U8, align_bytes=64, name="scales")
@@ -138,14 +137,16 @@ def tile_moe_res_glu_sigmoid_kernel(
         nc.sync.dma_start(gates, gate[0:P, :])
         nc.sync.dma_start(words2_i[:, E:, :], w2_i[E // 2 : E].rearrange("e s p b -> p (e s) b"))
 
-        y = keep.tile([P, E, N // P, C], F32, name="y")
+        y = keep.tile([P, E - 1, N // P, C], F32, name="y")
+        last = keep.tile([P, C], F32, name="last")
 
         def entries(a, b):
             return offsets[:, a // 16 : b // 16]
 
         def scatter(e, r):
+            values = y[:, e, r, :] if e < E - 1 else last[:]
             nc.vector.tensor_tensor(
-                windows[r][:].indirect(entries(e * C, (e + 1) * C)), y[:, e, r, :], gates[:, e * C : (e + 1) * C], MULT
+                windows[r][:].indirect(entries(e * C, (e + 1) * C)), values, gates[:, e * C : (e + 1) * C], MULT
             )
 
         head_codes = keep.tile([P, 2 * C], U32, align_bytes=64, name="head_codes")
@@ -233,7 +234,7 @@ def tile_moe_res_glu_sigmoid_kernel(
                         start=(s == 0),
                         stop=(s == 1),
                     )
-            if q == 1:
+            if q == 1 and e < E - 1:
                 nc.scalar.copy(y[:, e], y_banks[e][:])
 
         for n in range(AHEAD):
@@ -264,11 +265,33 @@ def tile_moe_res_glu_sigmoid_kernel(
         second_product(blocks - 1, *quantise(blocks - 1))
         residual = keep.tile([P, N // P, T], F32, align_bytes=64, name="residual", tag="words0")
         nc.sync.dma_start(residual[:], xr.rearrange("(r p) t -> p r t", p=P))
+        nc.scalar.copy(last[:], y_banks[E - 1][:, 0, :])
         scatter(E - 2, 1)
-        for r in range(N // P):
-            scatter(E - 1, r)
-            total = keep.tile([P, T], F32, name=f"total{r}")
-            for a, b in PIECES[r]:
-                piece = slice(a, b)
-                nc.vector.tensor_tensor(total[:, piece], windows[r][:, piece], residual[:, r, piece], ADD)
-                nc.sync.dma_start(out[r * P : (r + 1) * P, piece], total[:, piece])
+        sums = []
+        for b in range(TURNED):
+            bank = psum.tile([P, P], F32, name="sum_bank", tag=f"bank{b}")
+            nc.tensor.matmul(
+                bank[:], residual[:, 0, b * P : (b + 1) * P], ident[:], start=True, stop=False, is_transpose=True
+            )
+            sums.append(bank)
+        scatter(E - 1, 0)
+        nc.scalar.copy(last[:], y_banks[E - 1][:, 1, :])
+        across = keep.tile([P, TURNED, P], F32, name="across")
+        for b, bank in enumerate(sums):
+            nc.tensor.matmul(
+                bank[:], windows[0][:, b * P : (b + 1) * P], ident[:], start=False, stop=True, is_transpose=True
+            )
+            nc.scalar.copy(across[:, b, :], bank[:])
+        for tag, first_block in (("turned", 0), ("y_bank", TURNED // 2)):
+            back = psum.tile([P, TURNED // 2, P], F32, name="back", tag=tag)
+            for b in range(TURNED // 2):
+                nc.tensor.transpose(back[:, b, :], across[:, first_block + b, :], ident[:])
+            done = keep.tile([P, TURNED // 2 * P], F32, name=f"done{first_block}")
+            nc.scalar.copy(done[:], back[:].rearrange("p b c -> p (b c)"))
+            nc.scalar.dma_start(out[0:P, first_block * P : (first_block + TURNED // 2) * P], done[:])
+        for r, a, b in PIECES:
+            if (r, a) == (1, 0):
+                scatter(E - 1, 1)
+            total = keep.tile([P, b - a], F32, name=f"total{r}{a}")
+            nc.vector.tensor_tensor(total[:], windows[r][:, a:b], residual[:, r, a:b], ADD)
+            nc.sync.dma_start(out[r * P : (r + 1) * P, a:b], total[:])

@@ -20,17 +20,17 @@ ADD = mybir.AluOpType.add
 
 P = 128
 PACK = 4
+SCALE_ROWS = 4
 LOADS = (512, 384, 256, 128)
 CAST = 256
-SCALAR_SHARE = 8
+SCALAR_EIGHTHS = 3
 HALF = 512
 FIRST = 160
 LAG = 3
-EARLY = 1
 AHEAD = 3
-SPARE = 512
+EARLY_SCALES = 6
 TURNED = 6
-PIECES = ((0, 768, 1280), (1, 0, 512), (1, 512, 1024), (1, 1024, 1280))
+PIECES = ((0, TURNED * P, T), (1, 0, 512), (1, 512, 1024), (1, 1024, T))
 
 
 def tile_moe_res_glu_sigmoid_kernel(
@@ -42,29 +42,29 @@ def tile_moe_res_glu_sigmoid_kernel(
         ring = ctx.enter_context(tc.tile_pool(name="ring", bufs=4))
         psum = ctx.enter_context(tc.psum_pool(name="psum", bufs=1))
 
-        first = keep.tile([P, EARLY, 2, H], U8, align_bytes=64, name="first")
+        first = keep.tile([P, 1, 2, H], U8, align_bytes=64, name="first")
         first_i = first[:].rearrange("p e m i -> p (e m i)").bitcast(I32)
         nc.gpsimd.memset(first_i, 0)
-        first_i = first_i.rearrange("p (e m i) -> p e m i", e=EARLY, m=2)
-        warm = keep.tile([P, 1], F32, align_bytes=64, name="warm", tag="stage1")
-        nc.gpsimd.memset(warm[:], 0.0)
+        first_i = first_i.rearrange("p (e m i) -> p e m i", e=1, m=2)
+        seed = keep.tile([P, 1], F32, align_bytes=64, name="seed", tag="stage1")
+        nc.gpsimd.memset(seed[:], 0.0)
         zero = keep.tile([P, 1], F32, align_bytes=64, name="zero", tag="words0")
-        nc.scalar.copy(zero[:], warm[:])
+        nc.scalar.copy(zero[:], seed[:])
 
         codes = keep.tile([P, T], U32, align_bytes=64, name="codes")
         scales = keep.tile([P, T], U8, align_bytes=64, name="scales")
         nc.vector.memset(scales[:].bitcast(I32), 0)
-        rest = keep.tile([P, E - EARLY, 2, H], U8, align_bytes=64, name="rest")
+        rest = keep.tile([P, E - 1, 2, H], U8, align_bytes=64, name="rest")
         rest_i = rest[:].rearrange("p e m i -> p (e m i)").bitcast(I32)
         nc.vector.memset(rest_i, 0)
-        rest_i = rest_i.rearrange("p (e m i) -> p e m i", e=E - EARLY, m=2)
+        rest_i = rest_i.rearrange("p (e m i) -> p e m i", e=E - 1, m=2)
         planes2 = keep.tile([P, E, 2, N], U8, align_bytes=64, name="planes2")
         planes2_i = planes2[:].rearrange("p e s n -> p (e s n)").bitcast(I32)
         nc.vector.memset(planes2_i, 0)
         planes2_i = planes2_i.rearrange("p (e s n) -> p e s n", e=E, s=2)
         windows = []
         for r in range(N // P):
-            window = keep.tile([P, T + SPARE], F32, align_bytes=64, name=f"window{r}")
+            window = keep.tile([P, T + HALF], F32, align_bytes=64, name=f"window{r}")
             nc.scalar.copy(window[:, 0:T], zero[:].to_broadcast([P, T]))
             windows.append(window)
         ident = keep.tile([P, P], F32, name="ident")
@@ -79,11 +79,11 @@ def tile_moe_res_glu_sigmoid_kernel(
         nc.sync.dma_start(raw0[:], x_rows[:, :, 0 : LOADS[0]])
         raws = [(0, LOADS[0], raw0[:])]
         scale_loads = [
-            (first_i[r:P:32, :, m, :], rows[0:EARLY, 0, r:16:4, :].rearrange("e q i -> q e i"))
+            (first_i[r:P:32, :, m, :], rows[0:1, 0, r:16:SCALE_ROWS, :].rearrange("e q i -> q e i"))
             for m, rows in enumerate((s1_i, s3_i))
-            for r in range(4)
+            for r in range(SCALE_ROWS)
         ]
-        for dst, src in scale_loads[:6]:
+        for dst, src in scale_loads[:EARLY_SCALES]:
             nc.sync.dma_start(dst, src)
         raw1 = keep.tile([P, PACK * (T - LOADS[0])], F32, align_bytes=64, name="raw1", tag="stage1")
         t0 = LOADS[0]
@@ -93,7 +93,7 @@ def tile_moe_res_glu_sigmoid_kernel(
             nc.sync.dma_start(raw, x_rows[:, :, t0 : t0 + width])
             raws.append((t0, width, raw))
             t0 += width
-        for dst, src in scale_loads[6:]:
+        for dst, src in scale_loads[EARLY_SCALES:]:
             nc.sync.dma_start(dst, src)
         words0 = keep.tile([P, 2 * 2 * H], U8, align_bytes=64, name="words0", tag="words0")
         words0_i = words0[:].bitcast(I32).rearrange("p (m b) -> p m b", m=2)
@@ -104,7 +104,7 @@ def tile_moe_res_glu_sigmoid_kernel(
         for t0, width, raw in raws:
             for c in range(0, width, CAST):
                 end = min(c + CAST, width)
-                cut = c + 3 * (end - c) // SCALAR_SHARE
+                cut = c + SCALAR_EIGHTHS * (end - c) // 8
                 for copy, a, b in ((nc.scalar.copy, c, cut), (nc.vector.tensor_copy, cut, end)):
                     copy(
                         grouped[:, t0 + a : t0 + b, :].rearrange("p (c i) j -> p c j i", i=4),
@@ -122,20 +122,23 @@ def tile_moe_res_glu_sigmoid_kernel(
         words2 = keep.tile([P, E * 2 * 2 * N], U8, align_bytes=64, name="words2", tag="stage0")
         words2_i = words2[:].bitcast(I32).rearrange("p (x b) -> p x b", b=N // 2)
         gates = keep.tile([P, E * C], F32, align_bytes=64, name="gates", tag="grouped")[:]
-        for r in range(4):
+        for r in range(SCALE_ROWS):
             nc.sync.dma_start(
                 planes2_i[r:P:32].rearrange("q e s n -> q (e s) n"),
-                s2_i[:, :, r:16:4, :].rearrange("e s q n -> q (e s) n"),
+                s2_i[:, :, r:16:SCALE_ROWS, :].rearrange("e s q n -> q (e s) n"),
             )
         nc.sync.dma_start(words2_i[:, 0:E, :], w2_i[0 : E // 2].rearrange("e s p b -> p (e s) b"))
-        for r in range(4):
-            if r == 3:
+        nc.sync.dma_start(gates[:, 0:C], gate[0:P, 0:C])
+        for r in range(SCALE_ROWS):
+            if r == SCALE_ROWS - 1:
                 for m, src in enumerate((w1_i, w3_i)):
-                    nc.sync.dma_start(later_i[:, m], src[1:E, 0].rearrange("e p b -> p e b"))
+                    nc.sync.dma_start(later_i[:, m, 0 : E - 2], src[1 : E - 1, 0].rearrange("e p b -> p e b"))
             for m, src in ((1, s3_i), (0, s1_i)):
-                nc.sync.dma_start(rest_i[r:P:32, :, m, :], src[EARLY:E, 0, r:16:4, :].rearrange("e q i -> q e i"))
-        nc.sync.dma_start(gates, gate[0:P, :])
+                nc.sync.dma_start(rest_i[r:P:32, :, m, :], src[1:E, 0, r:16:SCALE_ROWS, :].rearrange("e q i -> q e i"))
+        for m, src in enumerate((w1_i, w3_i)):
+            nc.sync.dma_start(later_i[:, m, E - 2], src[E - 1, 0])
         nc.sync.dma_start(words2_i[:, E:, :], w2_i[E // 2 : E].rearrange("e s p b -> p (e s) b"))
+        nc.sync.dma_start(gates[:, C:], gate[0:P, C:])
 
         y = keep.tile([P, E - 1, N // P, C], F32, name="y")
         last = keep.tile([P, C], F32, name="last")
@@ -157,7 +160,7 @@ def tile_moe_res_glu_sigmoid_kernel(
         x_codes = [head_codes[:, 0:C], head_codes[:, C : 2 * C]]
         x_scales = [head_scales[:, 0:C], head_scales[:, C : 2 * C]]
 
-        LATE = ((codes, x_codes, U32, 2, 3), (scales, x_scales, U8, 2, 4), (codes, x_codes, U32, 3, 4))
+        late_gathers = ((codes, x_codes, U32, 2, 3), (scales, x_scales, U8, 2, 4), (codes, x_codes, U32, 3, 4))
         blocks = E * C // P
         steps = blocks * H // HALF
         banks = [(0, 1), (2, 3), (0, 4), (1, 5)]
@@ -173,10 +176,10 @@ def tile_moe_res_glu_sigmoid_kernel(
             pair = []
             for m in range(2):
                 bank = psum.tile([P, HALF], F32, name="bank", tag=f"bank{banks[n][m]}")
-                pair.append(bank[:].rearrange("p (w u k) -> p u w k", u=2, k=2))
-                table, at = (words0, m) if e == 0 else (later, m * (E - 1) + e - 1)
-                at = 2 * (at * H + s * HALF)
-                plane = first[:, e, m, i_cols] if e < EARLY else rest[:, e - EARLY, m, i_cols]
+                pair.append(bank[:].rearrange("p (w u v) -> p u w v", u=2, v=2))
+                table, matrix = (words0, m) if e == 0 else (later, m * (E - 1) + e - 1)
+                at = 2 * (matrix * H + s * HALF)
+                plane = first[:, 0, m, i_cols] if e == 0 else rest[:, e - 1, m, i_cols]
                 nc.tensor.matmul_mx(
                     out=bank[:],
                     lhsT=x_codes[e][:, slots].bitcast(FP8X4),
@@ -192,7 +195,7 @@ def tile_moe_res_glu_sigmoid_kernel(
                 sig = windows[(k - LAG) % 2][:, T : T + HALF]
             else:
                 sig = keep.tile([P, HALF], F32, align_bytes=64, name="sig", tag=f"even{k % 2}")[:]
-            sig_v = sig.rearrange("p (u w k) -> p u w k", u=2, k=2)
+            sig_v = sig.rearrange("p (u w v) -> p u w v", u=2, v=2)
             nc.scalar.activation(sig_v, pair[0], SIGMOID)
             ready[n] = (pair[1], sig_v)
 
@@ -245,10 +248,10 @@ def tile_moe_res_glu_sigmoid_kernel(
                 hs[k] = ring.tile([P, H], BF16, align_bytes=64, name="h")
             bank, sig_v = ready[n]
             nc.vector.tensor_tensor(
-                hs[k][:, s * HALF : (s + 1) * HALF].rearrange("p (u w k) -> p u w k", u=2, k=2), bank, sig_v, MULT
+                hs[k][:, s * HALF : (s + 1) * HALF].rearrange("p (u w v) -> p u w v", u=2, v=2), bank, sig_v, MULT
             )
             if k < LAG and s == 1:
-                table, kept, dtype, a, b = LATE[k]
+                table, kept, dtype, a, b = late_gathers[k]
                 late = keep.tile([P, (b - a) * C], dtype, align_bytes=64, name="late", tag=f"late{k}")
                 nc.vector.tensor_copy(late[:], table[:].indirect(entries(a * C, b * C)))
                 kept.extend(late[:, c * C : (c + 1) * C] for c in range(b - a))
@@ -263,10 +266,12 @@ def tile_moe_res_glu_sigmoid_kernel(
             if s == 0 and k > 0:
                 second_product(k - 1, *quantised)
         second_product(blocks - 1, *quantise(blocks - 1))
+
         residual = keep.tile([P, N // P, T], F32, align_bytes=64, name="residual", tag="words0")
         nc.sync.dma_start(residual[:], xr.rearrange("(r p) t -> p r t", p=P))
         nc.scalar.copy(last[:], y_banks[E - 1][:, 0, :])
         scatter(E - 2, 1)
+
         sums = []
         for b in range(TURNED):
             bank = psum.tile([P, P], F32, name="sum_bank", tag=f"bank{b}")

@@ -28,9 +28,8 @@ HALF = 512
 FIRST = 160
 LAG = 3
 AHEAD = 3
-EARLY_SCALES = 6
-TURNED = 6
-PIECES = ((0, TURNED * P, T), (1, 0, 512), (1, 512, 1024), (1, 1024, T))
+TURNED = 4
+PIECES = ((0, TURNED * P, T), (1, 0, 384), (1, 384, 768), (1, 768, 1024), (1, 1024, T))
 
 
 def tile_moe_res_glu_sigmoid_kernel(
@@ -44,12 +43,10 @@ def tile_moe_res_glu_sigmoid_kernel(
 
         first = keep.tile([P, 1, 2, H], U8, align_bytes=64, name="first")
         first_i = first[:].rearrange("p e m i -> p (e m i)").bitcast(I32)
-        nc.gpsimd.memset(first_i, 0)
+        nc.vector.memset(first_i, 0)
         first_i = first_i.rearrange("p (e m i) -> p e m i", e=1, m=2)
-        seed = keep.tile([P, 1], F32, align_bytes=64, name="seed", tag="stage1")
-        nc.gpsimd.memset(seed[:], 0.0)
-        zero = keep.tile([P, 1], F32, align_bytes=64, name="zero", tag="words0")
-        nc.scalar.copy(zero[:], seed[:])
+        zero = keep.tile([P, 1], F32, name="zero")
+        nc.gpsimd.memset(zero[:], 0.0)
 
         codes = keep.tile([P, T], U32, align_bytes=64, name="codes")
         scales = keep.tile([P, T], U8, align_bytes=64, name="scales")
@@ -78,13 +75,6 @@ def tile_moe_res_glu_sigmoid_kernel(
         raw0 = keep.tile([P, PACK, LOADS[0]], F32, align_bytes=64, name="raw0", tag="stage0")
         nc.sync.dma_start(raw0[:], x_rows[:, :, 0 : LOADS[0]])
         raws = [(0, LOADS[0], raw0[:])]
-        scale_loads = [
-            (first_i[r:P:32, :, m, :], rows[0:1, 0, r:16:SCALE_ROWS, :].rearrange("e q i -> q e i"))
-            for m, rows in enumerate((s1_i, s3_i))
-            for r in range(SCALE_ROWS)
-        ]
-        for dst, src in scale_loads[:EARLY_SCALES]:
-            nc.sync.dma_start(dst, src)
         raw1 = keep.tile([P, PACK * (T - LOADS[0])], F32, align_bytes=64, name="raw1", tag="stage1")
         t0 = LOADS[0]
         for width in LOADS[1:]:
@@ -93,12 +83,14 @@ def tile_moe_res_glu_sigmoid_kernel(
             nc.sync.dma_start(raw, x_rows[:, :, t0 : t0 + width])
             raws.append((t0, width, raw))
             t0 += width
-        for dst, src in scale_loads[EARLY_SCALES:]:
-            nc.sync.dma_start(dst, src)
-        words0 = keep.tile([P, 2 * 2 * H], U8, align_bytes=64, name="words0", tag="words0")
-        words0_i = words0[:].bitcast(I32).rearrange("p (m b) -> p m b", m=2)
-        for m, src in enumerate((w1_i, w3_i)):
-            nc.sync.dma_start(words0_i[:, m, :], src[0, 0])
+        for m, (queue, rows) in enumerate(((nc.sync, s1_i), (nc.gpsimd, s3_i))):
+            for r in range(SCALE_ROWS):
+                queue.dma_start(first_i[r:P:32, 0, m, :], rows[0, 0, r:16:SCALE_ROWS, :])
+        words0 = keep.tile([P, 2 * 2 * 2 * H], U8, align_bytes=64, name="words0", tag="words0")
+        words0_i = words0[:].bitcast(I32).rearrange("p (e m b) -> p e m b", e=2, m=2)
+        for e in range(2):
+            for m, src in enumerate((w1_i, w3_i)):
+                nc.sync.dma_start(words0_i[:, e, m, :], src[e, 0])
 
         grouped = keep.tile([P, T, PACK], BF16, align_bytes=64, name="grouped", tag="grouped")
         for t0, width, raw in raws:
@@ -117,8 +109,8 @@ def tile_moe_res_glu_sigmoid_kernel(
                     in_=grouped[:, cols, :].rearrange("p t j -> p (t j)"),
                 )
 
-        later = keep.tile([P, 2 * (E - 1) * 2 * H], U8, align_bytes=64, name="later", tag="stage1")
-        later_i = later[:].bitcast(I32).rearrange("p (m e b) -> p m e b", m=2, e=E - 1)
+        later = keep.tile([P, 2 * (E - 2) * 2 * H], U8, align_bytes=64, name="later", tag="stage1")
+        later_i = later[:].bitcast(I32).rearrange("p (e m b) -> p e m b", m=2, e=E - 2)
         words2 = keep.tile([P, E * 2 * 2 * N], U8, align_bytes=64, name="words2", tag="stage0")
         words2_i = words2[:].bitcast(I32).rearrange("p (x b) -> p x b", b=N // 2)
         gates = keep.tile([P, E * C], F32, align_bytes=64, name="gates", tag="grouped")[:]
@@ -127,18 +119,18 @@ def tile_moe_res_glu_sigmoid_kernel(
                 planes2_i[r:P:32].rearrange("q e s n -> q (e s) n"),
                 s2_i[:, :, r:16:SCALE_ROWS, :].rearrange("e s q n -> q (e s) n"),
             )
-        nc.sync.dma_start(words2_i[:, 0:E, :], w2_i[0 : E // 2].rearrange("e s p b -> p (e s) b"))
-        nc.sync.dma_start(gates[:, 0:C], gate[0:P, 0:C])
         for r in range(SCALE_ROWS):
-            if r == SCALE_ROWS - 1:
-                for m, src in enumerate((w1_i, w3_i)):
-                    nc.sync.dma_start(later_i[:, m, 0 : E - 2], src[1 : E - 1, 0].rearrange("e p b -> p e b"))
             for m, src in ((1, s3_i), (0, s1_i)):
                 nc.sync.dma_start(rest_i[r:P:32, :, m, :], src[1:E, 0, r:16:SCALE_ROWS, :].rearrange("e q i -> q e i"))
-        for m, src in enumerate((w1_i, w3_i)):
-            nc.sync.dma_start(later_i[:, m, E - 2], src[E - 1, 0])
-        nc.sync.dma_start(words2_i[:, E:, :], w2_i[E // 2 : E].rearrange("e s p b -> p (e s) b"))
-        nc.sync.dma_start(gates[:, C:], gate[0:P, C:])
+        for half in range(2):
+            nc.sync.dma_start(
+                words2_i[:, E * half : E * (half + 1), :],
+                w2_i[2 * half : 2 * half + 2].rearrange("e s p b -> p (e s) b"),
+            )
+            for m, src in ((1, w3_i), (0, w1_i)):
+                nc.sync.dma_start(later_i[:, half, m], src[2 + half, 0])
+            a, b = ((0, C), (C, E * C))[half]
+            nc.sync.dma_start(gates[:, a:b], gate[0:P, a:b])
 
         y = keep.tile([P, E - 1, N // P, C], F32, name="y")
         last = keep.tile([P, C], F32, name="last")
@@ -160,7 +152,10 @@ def tile_moe_res_glu_sigmoid_kernel(
         x_codes = [head_codes[:, 0:C], head_codes[:, C : 2 * C]]
         x_scales = [head_scales[:, 0:C], head_scales[:, C : 2 * C]]
 
-        late_gathers = ((codes, x_codes, U32, 2, 3), (scales, x_scales, U8, 2, 4), (codes, x_codes, U32, 3, 4))
+        late_gathers = ((scales, x_scales, U8, 2, 3), (codes, x_codes, U32, 3, 4), (scales, x_scales, U8, 3, 4))
+        third = keep.tile([P, C], U32, align_bytes=64, name="third")
+        nc.vector.tensor_copy(third[:], codes[:].indirect(entries(2 * C, 3 * C)))
+        x_codes.append(third[:])
         blocks = E * C // P
         steps = blocks * H // HALF
         banks = [(0, 1), (2, 3), (0, 4), (1, 5)]
@@ -177,8 +172,8 @@ def tile_moe_res_glu_sigmoid_kernel(
             for m in range(2):
                 bank = psum.tile([P, HALF], F32, name="bank", tag=f"bank{banks[n][m]}")
                 pair.append(bank[:].rearrange("p (w u v) -> p u w v", u=2, v=2))
-                table, matrix = (words0, m) if e == 0 else (later, m * (E - 1) + e - 1)
-                at = 2 * (matrix * H + s * HALF)
+                table = words0 if e < 2 else later
+                at = 2 * ((2 * (e % 2) + m) * H + s * HALF)
                 plane = first[:, 0, m, i_cols] if e == 0 else rest[:, e - 1, m, i_cols]
                 nc.tensor.matmul_mx(
                     out=bank[:],
@@ -190,7 +185,7 @@ def tile_moe_res_glu_sigmoid_kernel(
                     stop=True,
                 )
             if k < LAG and s == 1:
-                sig = keep.tile([P, HALF], F32, align_bytes=64, name="sig_once", tag=f"late{k}")[:]
+                sig = keep.tile([P, HALF], F32, align_bytes=64, name="sig_once", tag=f"odd{k}")[:]
             elif s == 1:
                 sig = windows[(k - LAG) % 2][:, T : T + HALF]
             else:
@@ -216,7 +211,7 @@ def tile_moe_res_glu_sigmoid_kernel(
             turned_h[k] = hg
 
         def quantise(k):
-            h_codes = keep.tile([P, 2 * P], U32, align_bytes=64, name="h_codes", tag=f"even{(k + 1) % 2}")
+            h_codes = ring.tile([P, 2 * P], U32, align_bytes=64, name="h_codes")
             h_scales = ring.tile([P, 2 * P], U8, align_bytes=64, name="h_scales")
             nc.vector.quantize_mx(out=h_codes[:].bitcast(FP8X4), scales=h_scales[:], in_=turned_h[k].bitcast(BF16))
             return h_codes, h_scales
@@ -245,20 +240,23 @@ def tile_moe_res_glu_sigmoid_kernel(
         for n in range(steps):
             k, s = divmod(n, 2)
             if s == 0:
-                hs[k] = ring.tile([P, H], BF16, align_bytes=64, name="h")
+                if k < LAG:
+                    hs[k] = keep.tile([P, H], BF16, align_bytes=64, name="h_once", tag=f"late{k}")
+                else:
+                    hs[k] = ring.tile([P, H], BF16, align_bytes=64, name="h")
             bank, sig_v = ready[n]
             nc.vector.tensor_tensor(
                 hs[k][:, s * HALF : (s + 1) * HALF].rearrange("p (u w v) -> p u w v", u=2, v=2), bank, sig_v, MULT
             )
+            if s == 1:
+                if k >= LAG:
+                    scatter(*divmod(k - LAG, 2))
+                turn(k)
             if k < LAG and s == 1:
                 table, kept, dtype, a, b = late_gathers[k]
                 late = keep.tile([P, (b - a) * C], dtype, align_bytes=64, name="late", tag=f"late{k}")
                 nc.vector.tensor_copy(late[:], table[:].indirect(entries(a * C, b * C)))
                 kept.extend(late[:, c * C : (c + 1) * C] for c in range(b - a))
-            if s == 1:
-                if k >= LAG:
-                    scatter(*divmod(k - LAG, 2))
-                turn(k)
             if s == 0 and k > 0:
                 quantised = quantise(k - 1)
             if n + AHEAD < steps:
@@ -287,13 +285,12 @@ def tile_moe_res_glu_sigmoid_kernel(
                 bank[:], windows[0][:, b * P : (b + 1) * P], ident[:], start=False, stop=True, is_transpose=True
             )
             nc.scalar.copy(across[:, b, :], bank[:])
-        for tag, first_block in (("turned", 0), ("y_bank", TURNED // 2)):
-            back = psum.tile([P, TURNED // 2, P], F32, name="back", tag=tag)
-            for b in range(TURNED // 2):
-                nc.tensor.transpose(back[:, b, :], across[:, first_block + b, :], ident[:])
-            done = keep.tile([P, TURNED // 2 * P], F32, name=f"done{first_block}")
-            nc.scalar.copy(done[:], back[:].rearrange("p b c -> p (b c)"))
-            nc.scalar.dma_start(out[0:P, first_block * P : (first_block + TURNED // 2) * P], done[:])
+        back = psum.tile([P, TURNED, P], F32, name="back", tag="turned")
+        for b in range(TURNED):
+            nc.tensor.transpose(back[:, b, :], across[:, b, :], ident[:])
+        done = keep.tile([P, TURNED * P], F32, name="done")
+        nc.scalar.copy(done[:], back[:].rearrange("p b c -> p (b c)"))
+        nc.scalar.dma_start(out[0:P, 0 : TURNED * P], done[:])
         for r, a, b in PIECES:
             if (r, a) == (1, 0):
                 scatter(E - 1, 1)

@@ -41,20 +41,20 @@ def tile_moe_res_glu_sigmoid_kernel(
         ring = ctx.enter_context(tc.tile_pool(name="ring", bufs=4))
         psum = ctx.enter_context(tc.psum_pool(name="psum", bufs=1))
 
-        first = keep.tile([P, 1, 2, H], U8, align_bytes=64, name="first")
+        first = keep.tile([P, 2, 2, H], U8, align_bytes=64, name="first")
         first_i = first[:].rearrange("p e m i -> p (e m i)").bitcast(I32)
         nc.vector.memset(first_i, 0)
-        first_i = first_i.rearrange("p (e m i) -> p e m i", e=1, m=2)
+        first_i = first_i.rearrange("p (e m i) -> p e m i", e=2, m=2)
         zero = keep.tile([P, 1], F32, name="zero")
         nc.gpsimd.memset(zero[:], 0.0)
 
         codes = keep.tile([P, T], U32, align_bytes=64, name="codes")
         scales = keep.tile([P, T], U8, align_bytes=64, name="scales")
         nc.vector.memset(scales[:].bitcast(I32), 0)
-        rest = keep.tile([P, E - 1, 2, H], U8, align_bytes=64, name="rest")
+        rest = keep.tile([P, 2, 2, H], U8, align_bytes=64, name="rest")
         rest_i = rest[:].rearrange("p e m i -> p (e m i)").bitcast(I32)
         nc.vector.memset(rest_i, 0)
-        rest_i = rest_i.rearrange("p (e m i) -> p e m i", e=E - 1, m=2)
+        rest_i = rest_i.rearrange("p (e m i) -> p e m i", e=2, m=2)
         planes2 = keep.tile([P, E, 2, N], U8, align_bytes=64, name="planes2")
         planes2_i = planes2[:].rearrange("p e s n -> p (e s n)").bitcast(I32)
         nc.vector.memset(planes2_i, 0)
@@ -85,7 +85,7 @@ def tile_moe_res_glu_sigmoid_kernel(
             t0 += width
         for m, (queue, rows) in enumerate(((nc.sync, s1_i), (nc.gpsimd, s3_i))):
             for r in range(SCALE_ROWS):
-                queue.dma_start(first_i[r:P:32, 0, m, :], rows[0, 0, r:16:SCALE_ROWS, :])
+                queue.dma_start(first_i[r:P:32, :, m, :], rows[0:2, 0, r:16:SCALE_ROWS, :].rearrange("e q i -> q e i"))
         words0 = keep.tile([P, 2 * 2 * 2 * H], U8, align_bytes=64, name="words0", tag="words0")
         words0_i = words0[:].bitcast(I32).rearrange("p (e m b) -> p e m b", e=2, m=2)
         for e in range(2):
@@ -119,18 +119,17 @@ def tile_moe_res_glu_sigmoid_kernel(
                 planes2_i[r:P:32].rearrange("q e s n -> q (e s) n"),
                 s2_i[:, :, r:16:SCALE_ROWS, :].rearrange("e s q n -> q (e s) n"),
             )
+        nc.sync.dma_start(words2_i[:, 0:E, :], w2_i[0:2].rearrange("e s p b -> p (e s) b"))
+        nc.sync.dma_start(gates[:, 0:C], gate[0:P, 0:C])
+        for m, src in ((1, w3_i), (0, w1_i)):
+            nc.sync.dma_start(later_i[:, 0, m], src[2, 0])
         for r in range(SCALE_ROWS):
             for m, src in ((1, s3_i), (0, s1_i)):
-                nc.sync.dma_start(rest_i[r:P:32, :, m, :], src[1:E, 0, r:16:SCALE_ROWS, :].rearrange("e q i -> q e i"))
-        for half in range(2):
-            nc.sync.dma_start(
-                words2_i[:, E * half : E * (half + 1), :],
-                w2_i[2 * half : 2 * half + 2].rearrange("e s p b -> p (e s) b"),
-            )
-            for m, src in ((1, w3_i), (0, w1_i)):
-                nc.sync.dma_start(later_i[:, half, m], src[2 + half, 0])
-            a, b = ((0, C), (C, E * C))[half]
-            nc.sync.dma_start(gates[:, a:b], gate[0:P, a:b])
+                nc.sync.dma_start(rest_i[r:P:32, :, m, :], src[2:E, 0, r:16:SCALE_ROWS, :].rearrange("e q i -> q e i"))
+        nc.sync.dma_start(gates[:, C:], gate[0:P, C:])
+        for m, src in ((1, w3_i), (0, w1_i)):
+            nc.sync.dma_start(later_i[:, 1, m], src[3, 0])
+        nc.sync.dma_start(words2_i[:, E:, :], w2_i[2:E].rearrange("e s p b -> p (e s) b"))
 
         y = keep.tile([P, E - 1, N // P, C], F32, name="y")
         last = keep.tile([P, C], F32, name="last")
@@ -170,11 +169,12 @@ def tile_moe_res_glu_sigmoid_kernel(
             i_cols = slice(s * HALF, (s + 1) * HALF)
             pair = []
             for m in range(2):
-                bank = psum.tile([P, HALF], F32, name="bank", tag=f"bank{banks[n][m]}")
+                tag = "turned" if (n, m) == (steps // 2, 0) else f"bank{banks[n][m]}"
+                bank = psum.tile([P, HALF], F32, name="bank", tag=tag)
                 pair.append(bank[:].rearrange("p (w u v) -> p u w v", u=2, v=2))
                 table = words0 if e < 2 else later
                 at = 2 * ((2 * (e % 2) + m) * H + s * HALF)
-                plane = first[:, 0, m, i_cols] if e == 0 else rest[:, e - 1, m, i_cols]
+                plane = (first, rest)[e // 2][:, e % 2, m, i_cols]
                 nc.tensor.matmul_mx(
                     out=bank[:],
                     lhsT=x_codes[e][:, slots].bitcast(FP8X4),
@@ -184,8 +184,8 @@ def tile_moe_res_glu_sigmoid_kernel(
                     start=True,
                     stop=True,
                 )
-            if k < LAG and s == 1:
-                sig = keep.tile([P, HALF], F32, align_bytes=64, name="sig_once", tag=f"odd{k}")[:]
+            if k < LAG:
+                sig = keep.tile([P, HALF], F32, align_bytes=64, name="sig_once", tag=f"{('late', 'odd')[s]}{k}")[:]
             elif s == 1:
                 sig = windows[(k - LAG) % 2][:, T : T + HALF]
             else:
@@ -219,7 +219,7 @@ def tile_moe_res_glu_sigmoid_kernel(
         def second_product(k, h_codes, h_scales):
             e, q = divmod(k, C // P)
             if q == 0:
-                y_banks[e] = psum.tile([P, N // P, C], F32, name="y_bank")
+                y_banks[e] = psum.tile([P, N // P, C], F32, name="y_bank", tag="turned" if e == 1 else "y_bank")
             for r in range(N // P):
                 for s in range(2):
                     at = 2 * ((2 * e + s) * N + r * P)
@@ -240,10 +240,7 @@ def tile_moe_res_glu_sigmoid_kernel(
         for n in range(steps):
             k, s = divmod(n, 2)
             if s == 0:
-                if k < LAG:
-                    hs[k] = keep.tile([P, H], BF16, align_bytes=64, name="h_once", tag=f"late{k}")
-                else:
-                    hs[k] = ring.tile([P, H], BF16, align_bytes=64, name="h")
+                hs[k] = ring.tile([P, H], BF16, align_bytes=64, name="h")
             bank, sig_v = ready[n]
             nc.vector.tensor_tensor(
                 hs[k][:, s * HALF : (s + 1) * HALF].rearrange("p (u w v) -> p u w v", u=2, v=2), bank, sig_v, MULT

@@ -41,13 +41,17 @@ def tile_moe_res_glu_sigmoid_kernel(
         ring = ctx.enter_context(tc.tile_pool(name="ring", bufs=4))
         psum = ctx.enter_context(tc.psum_pool(name="psum", bufs=1))
 
+        zeros = []
+        for tag in ("words0", "zero"):
+            zero = keep.tile([P, 1], F32, align_bytes=64, name="zero", tag=tag)
+            nc.gpsimd.memset(zero[:], 0.0)
+            zeros.append(zero)
+
         first = keep.tile([P, 2, 2, H], U8, align_bytes=64, name="first")
         first_i = first[:].rearrange("p e m i -> p (e m i)").bitcast(I32)
-        nc.vector.memset(first_i, 0)
+        for e, engine in enumerate((nc.vector, nc.gpsimd)):
+            engine.memset(first_i[:, e * H // 2 : (e + 1) * H // 2], 0)
         first_i = first_i.rearrange("p (e m i) -> p e m i", e=2, m=2)
-        zero = keep.tile([P, 1], F32, name="zero")
-        nc.gpsimd.memset(zero[:], 0.0)
-
         codes = keep.tile([P, T], U32, align_bytes=64, name="codes")
         scales = keep.tile([P, T], U8, align_bytes=64, name="scales")
         nc.vector.memset(scales[:].bitcast(I32), 0)
@@ -62,7 +66,7 @@ def tile_moe_res_glu_sigmoid_kernel(
         windows = []
         for r in range(N // P):
             window = keep.tile([P, T + HALF], F32, align_bytes=64, name=f"window{r}")
-            nc.scalar.copy(window[:, 0:T], zero[:].to_broadcast([P, T]))
+            nc.scalar.copy(window[:, 0:T], zeros[r][:].to_broadcast([P, T]))
             windows.append(window)
         ident = keep.tile([P, P], F32, name="ident")
         make_identity(nc, ident[:])

@@ -27,7 +27,8 @@ SCALAR_EIGHTHS = 3
 HALF = 512
 FIRST = 160
 LAG = 3
-AHEAD = 3
+SHARED = 3
+AHEAD = 4
 TURNED = 4
 PIECES = ((0, TURNED * P, T), (1, 0, 384), (1, 384, 768), (1, 768, 1024), (1, 1024, T))
 
@@ -65,7 +66,7 @@ def tile_moe_res_glu_sigmoid_kernel(
         planes2_i = planes2_i.rearrange("p (e s n) -> p e s n", e=E, s=2)
         windows = []
         for r in range(N // P):
-            window = keep.tile([P, T + HALF], F32, align_bytes=64, name=f"window{r}")
+            window = keep.tile([P, T + 2 * P], F32, align_bytes=64, name=f"window{r}")
             nc.scalar.copy(window[:, 0:T], zeros[r][:].to_broadcast([P, T]))
             windows.append(window)
         ident = keep.tile([P, P], F32, name="ident")
@@ -142,10 +143,11 @@ def tile_moe_res_glu_sigmoid_kernel(
             return offsets[:, a // 16 : b // 16]
 
         def scatter(e, r):
-            values = y[:, e, r, :] if e < E - 1 else last[:]
-            nc.vector.tensor_tensor(
-                windows[r][:].indirect(entries(e * C, (e + 1) * C)), values, gates[:, e * C : (e + 1) * C], MULT
-            )
+            window = windows[r][:].indirect(entries(e * C, (e + 1) * C))
+            if e < E - 1:
+                nc.vector.tensor_copy(window, gated[e, r][:])
+            else:
+                nc.vector.tensor_tensor(window, last[:], gates[:, e * C : (e + 1) * C], MULT)
 
         head_codes = keep.tile([P, 2 * C], U32, align_bytes=64, name="head_codes")
         head_scales = keep.tile([P, 2 * C], U8, align_bytes=64, name="head_scales")
@@ -161,10 +163,15 @@ def tile_moe_res_glu_sigmoid_kernel(
         x_codes.append(third[:])
         blocks = E * C // P
         steps = blocks * H // HALF
-        banks = [(0, 1), (2, 3), (0, 4), (1, 5)]
-        for n in range(len(banks), steps):
-            banks.append(banks[n - AHEAD][::-1])
-        ready, hs, turned_h, y_banks = {}, {}, {}, {}
+
+        def bank_tags(k, s):
+            if s == 1:
+                return f"bank{k % 2}", f"bank{2 + k % 2}"
+            if k == 1:
+                return "bank4", "y_bank1"
+            return (f"y_bank{(k // 2 - 1) % 2}" if k > 0 and k % 2 == 0 else "bank4"), "bank5"
+
+        ready, hs, turned_h, y_banks, gated = {}, {}, {}, {}, {}
 
         def first_products(n):
             k, s = divmod(n, 2)
@@ -173,8 +180,7 @@ def tile_moe_res_glu_sigmoid_kernel(
             i_cols = slice(s * HALF, (s + 1) * HALF)
             pair = []
             for m in range(2):
-                tag = "turned" if (n, m) == (steps // 2, 0) else f"bank{banks[n][m]}"
-                bank = psum.tile([P, HALF], F32, name="bank", tag=tag)
+                bank = psum.tile([P, HALF], F32, name="bank", tag=bank_tags(k, s)[m])
                 pair.append(bank[:].rearrange("p (w u v) -> p u w v", u=2, v=2))
                 table = words0 if e < 2 else later
                 at = 2 * ((2 * (e % 2) + m) * H + s * HALF)
@@ -188,42 +194,60 @@ def tile_moe_res_glu_sigmoid_kernel(
                     start=True,
                     stop=True,
                 )
-            if k < LAG:
-                sig = keep.tile([P, HALF], F32, align_bytes=64, name="sig_once", tag=f"{('late', 'odd')[s]}{k}")[:]
-            elif s == 1:
-                sig = windows[(k - LAG) % 2][:, T : T + HALF]
-            else:
-                sig = keep.tile([P, HALF], F32, align_bytes=64, name="sig", tag=f"even{k % 2}")[:]
+            tag = f"late{k}" if k < LAG and s == 0 else f"{('even', 'odd')[s]}{k % 2}"
+            sig = keep.tile([P, HALF], F32, align_bytes=64, name="sig", tag=tag)[:]
             sig_v = sig.rearrange("p (u w v) -> p u w v", u=2, v=2)
             nc.scalar.activation(sig_v, pair[0], SIGMOID)
-            ready[n] = (pair[1], sig_v)
+            if s == 0 and k >= SHARED:
+                plain = keep.tile([P, HALF], F32, align_bytes=64, name="plain", tag=f"plain{k % 3}")[:]
+                nc.scalar.copy(plain.rearrange("p (u w v) -> p u w v", u=2, v=2), pair[1])
+                ready[n] = (plain, sig)
+            else:
+                ready[n] = (pair[1], sig_v)
+
+        def product(n):
+            k, s = divmod(n, 2)
+            if s == 0 and k >= SHARED:
+                h = keep.tile([P, HALF], BF16, align_bytes=64, name="h0", tag=f"swap{k % 2}")
+                nc.gpsimd.tensor_tensor(h[:], *ready[n], MULT)
+            else:
+                h = ring.tile([P, HALF], BF16, align_bytes=64, name="h1")
+                nc.vector.tensor_tensor(h[:].rearrange("p (u w v) -> p u w v", u=2, v=2), *ready[n], MULT)
+            hs[n] = h
+
+        def weigh(k):
+            e, r = divmod(k - 2, 2)
+            tag = f"plain{(k + 1) % 3}" if k + 1 < blocks else f"swap{(k + 1) % 2}"
+            gated[e, r] = keep.tile([P, C], F32, align_bytes=64, name="gated", tag=tag)
+            nc.gpsimd.tensor_tensor(gated[e, r][:], y[:, e, r, :], gates[:, e * C : (e + 1) * C], MULT)
 
         def turn(k):
-            tag = f"bank{banks[2 * k + 2][0]}" if 2 * k + 2 < steps else "turned"
+            tag = f"bank{(k + 1) % 2}"
             turned = psum.tile([P, 2, 2, P], F32, name="turned", tag=tag)
             for s in range(2):
                 for u in range(2):
-                    b = 2 * s + u
-                    nc.tensor.transpose(turned[:, s, u, :], hs[k][:].bitcast(F32)[:, b * P : (b + 1) * P], ident[:])
-            if k == blocks - 1:
-                hg = windows[1][:, T : T + HALF]
+                    nc.tensor.transpose(turned[:, s, u, :], hs[2 * k + s][:].bitcast(F32)[:, u * P : (u + 1) * P], ident[:])
+            if k + 1 >= LAG:
+                low = windows[(k + 1 - LAG) % 2][:, T : T + 2 * P]
             else:
-                hg = ring.tile([P, HALF], F32, align_bytes=64, name="hg")[:]
-            nc.scalar.copy(
-                hg.rearrange("p (s c u) -> p s c u", s=2, u=2), turned[:].rearrange("p s u c -> p s c u")
-            )
-            turned_h[k] = hg
+                low = ring.tile([P, 2 * P], F32, align_bytes=64, name="low")[:]
+            high = keep.tile([P, 2 * P], F32, align_bytes=64, name="high", tag=f"swap{k % 2}")[:]
+            for s, half in enumerate((low, high)):
+                nc.scalar.copy(half.rearrange("p (c u) -> p c u", u=2), turned[:, s].rearrange("p u c -> p c u"))
+            turned_h[k] = (low, high)
 
         def quantise(k):
             h_codes = ring.tile([P, 2 * P], U32, align_bytes=64, name="h_codes")
             h_scales = ring.tile([P, 2 * P], U8, align_bytes=64, name="h_scales")
-            nc.vector.quantize_mx(out=h_codes[:].bitcast(FP8X4), scales=h_scales[:], in_=turned_h[k].bitcast(BF16))
+            for s, half in enumerate(turned_h[k]):
+                cols = slice(s * P, (s + 1) * P)
+                nc.vector.quantize_mx(out=h_codes[:, cols].bitcast(FP8X4), scales=h_scales[:, cols], in_=half.bitcast(BF16))
             return h_codes, h_scales
 
         def second_product(k, h_codes, h_scales):
             e, q = divmod(k, C // P)
             if q == 0:
-                y_banks[e] = psum.tile([P, N // P, C], F32, name="y_bank", tag="turned" if e == 1 else "y_bank")
+                y_banks[e] = psum.tile([P, N // P, C], F32, name="y_bank", tag=f"y_bank{e % 2}")
             for r in range(N // P):
                 for s in range(2):
                     at = 2 * ((2 * e + s) * N + r * P)
@@ -241,29 +265,29 @@ def tile_moe_res_glu_sigmoid_kernel(
 
         for n in range(AHEAD):
             first_products(n)
-        for n in range(steps):
-            k, s = divmod(n, 2)
-            if s == 0:
-                hs[k] = ring.tile([P, H], BF16, align_bytes=64, name="h")
-            bank, sig_v = ready[n]
-            nc.vector.tensor_tensor(
-                hs[k][:, s * HALF : (s + 1) * HALF].rearrange("p (u w v) -> p u w v", u=2, v=2), bank, sig_v, MULT
-            )
-            if s == 1:
-                if k >= LAG:
-                    scatter(*divmod(k - LAG, 2))
-                turn(k)
-            if k < LAG and s == 1:
+        for k in range(blocks):
+            if k < SHARED:
+                product(2 * k)
+            if k > 0:
+                quantised = quantise(k - 1)
+            if SHARED <= k + 1 < blocks:
+                product(2 * k + 2)
+            if k > 0:
+                second_product(k - 1, *quantised)
+            if k >= 2:
+                weigh(k)
+            product(2 * k + 1)
+            if k >= LAG:
+                scatter(*divmod(k - LAG, 2))
+            turn(k)
+            if k < LAG:
                 table, kept, dtype, a, b = late_gathers[k]
                 late = keep.tile([P, (b - a) * C], dtype, align_bytes=64, name="late", tag=f"late{k}")
                 nc.vector.tensor_copy(late[:], table[:].indirect(entries(a * C, b * C)))
                 kept.extend(late[:, c * C : (c + 1) * C] for c in range(b - a))
-            if s == 0 and k > 0:
-                quantised = quantise(k - 1)
-            if n + AHEAD < steps:
-                first_products(n + AHEAD)
-            if s == 0 and k > 0:
-                second_product(k - 1, *quantised)
+            for n in (2 * k + AHEAD, 2 * k + AHEAD + 1):
+                if n < steps:
+                    first_products(n)
         second_product(blocks - 1, *quantise(blocks - 1))
 
         residual = keep.tile([P, N // P, T], F32, align_bytes=64, name="residual", tag="words0")
@@ -286,7 +310,7 @@ def tile_moe_res_glu_sigmoid_kernel(
                 bank[:], windows[0][:, b * P : (b + 1) * P], ident[:], start=False, stop=True, is_transpose=True
             )
             nc.scalar.copy(across[:, b, :], bank[:])
-        back = psum.tile([P, TURNED, P], F32, name="back", tag="turned")
+        back = psum.tile([P, TURNED, P], F32, name="back", tag="bank4")
         for b in range(TURNED):
             nc.tensor.transpose(back[:, b, :], across[:, b, :], ident[:])
         done = keep.tile([P, TURNED * P], F32, name="done")

@@ -260,8 +260,6 @@ def tile_moe_res_glu_sigmoid_kernel(
                         start=(s == 0),
                         stop=(s == 1),
                     )
-            if q == 1 and e < E - 1:
-                nc.scalar.copy(y[:, e], y_banks[e][:])
 
         for n in range(AHEAD):
             first_products(n)
@@ -274,9 +272,12 @@ def tile_moe_res_glu_sigmoid_kernel(
                 product(2 * k + 2)
             if k > 0:
                 second_product(k - 1, *quantised)
-            if k >= 2:
-                weigh(k)
             product(2 * k + 1)
+            if k >= 2 and k % 2 == 0:
+                e = k // 2 - 1
+                both = gates[:, e * C : (e + 1) * C].unsqueeze(1).to_broadcast([P, N // P, C])
+                nc.vector.tensor_tensor(y[:, e], y_banks[e][:], both, MULT)
+                gated[e, 0], gated[e, 1] = y[:, e, 0, :], y[:, e, 1, :]
             if k >= LAG:
                 scatter(*divmod(k - LAG, 2))
             turn(k)

@@ -171,7 +171,7 @@ def tile_moe_res_glu_sigmoid_kernel(
                 return "bank4", "y_bank1"
             return (f"y_bank{(k // 2 - 1) % 2}" if k > 0 and k % 2 == 0 else "bank4"), "bank5"
 
-        ready, hs, turned_h, y_banks, gated = {}, {}, {}, {}, {}
+        ready, hs, turned_h, y_banks, gated, extra = {}, {}, {}, {}, {}, {}
 
         def first_products(n):
             k, s = divmod(n, 2)
@@ -202,31 +202,39 @@ def tile_moe_res_glu_sigmoid_kernel(
                 plain = keep.tile([P, HALF], F32, align_bytes=64, name="plain", tag=f"plain{k % 3}")[:]
                 nc.scalar.copy(plain.rearrange("p (u w v) -> p u w v", u=2, v=2), pair[1])
                 ready[n] = (plain, sig)
+            elif k >= SHARED and k % 2 == 1:
+                more = keep.tile([P, HALF // 2], F32, align_bytes=64, name="more", tag="more")[:]
+                nc.scalar.copy(more.rearrange("p (w v) -> p w v", v=2), pair[1][:, 0])
+                extra[k] = (more, sig[:, 0 : HALF // 2])
+                ready[n] = (pair[1][:, 1], sig_v[:, 1])
             else:
                 ready[n] = (pair[1], sig_v)
 
         def product(n):
             k, s = divmod(n, 2)
             if s == 0 and k >= SHARED:
-                h = keep.tile([P, HALF], BF16, align_bytes=64, name="h0", tag=f"swap{k % 2}")
-                nc.gpsimd.tensor_tensor(h[:], *ready[n], MULT)
+                h = keep.tile([P, HALF + HALF // 2], BF16, align_bytes=64, name="h0", tag=f"swap{k % 2}")
+                nc.gpsimd.tensor_tensor(h[:, 0:HALF], *ready[n], MULT)
+                quarters = [h[:, 0 : HALF // 2], h[:, HALF // 2 : HALF]]
+                if k in extra:
+                    nc.gpsimd.tensor_tensor(h[:, HALF:], *extra[k], MULT)
+                    quarters.append(h[:, HALF:])
+            elif s == 1 and k in extra:
+                h = ring.tile([P, HALF // 2], BF16, align_bytes=64, name="h1")
+                nc.vector.tensor_tensor(h[:].rearrange("p (w v) -> p w v", v=2), *ready[n], MULT)
+                quarters = [h[:]]
             else:
                 h = ring.tile([P, HALF], BF16, align_bytes=64, name="h1")
                 nc.vector.tensor_tensor(h[:].rearrange("p (u w v) -> p u w v", u=2, v=2), *ready[n], MULT)
-            hs[n] = h
-
-        def weigh(k):
-            e, r = divmod(k - 2, 2)
-            tag = f"plain{(k + 1) % 3}" if k + 1 < blocks else f"swap{(k + 1) % 2}"
-            gated[e, r] = keep.tile([P, C], F32, align_bytes=64, name="gated", tag=tag)
-            nc.gpsimd.tensor_tensor(gated[e, r][:], y[:, e, r, :], gates[:, e * C : (e + 1) * C], MULT)
+                quarters = [h[:, 0 : HALF // 2], h[:, HALF // 2 : HALF]]
+            hs[n] = quarters
 
         def turn(k):
             tag = f"bank{(k + 1) % 2}"
             turned = psum.tile([P, 2, 2, P], F32, name="turned", tag=tag)
             for s in range(2):
                 for u in range(2):
-                    nc.tensor.transpose(turned[:, s, u, :], hs[2 * k + s][:].bitcast(F32)[:, u * P : (u + 1) * P], ident[:])
+                    nc.tensor.transpose(turned[:, s, u, :], (hs[2 * k] + hs[2 * k + 1])[2 * s + u].bitcast(F32), ident[:])
             if k + 1 >= LAG:
                 low = windows[(k + 1 - LAG) % 2][:, T : T + 2 * P]
             else:

@@ -28,6 +28,7 @@ HALF = 512
 FIRST = 160
 LAG = 3
 SHARED = 3
+GATED = 2
 AHEAD = 4
 TURNED = 4
 PIECES = ((0, TURNED * P, T), (1, 0, 384), (1, 384, 768), (1, 768, 1024), (1, 1024, T))
@@ -90,7 +91,8 @@ def tile_moe_res_glu_sigmoid_kernel(
             t0 += width
         for m, (queue, rows) in enumerate(((nc.sync, s1_i), (nc.gpsimd, s3_i))):
             for r in range(SCALE_ROWS):
-                queue.dma_start(first_i[r:P:32, :, m, :], rows[0:2, 0, r:16:SCALE_ROWS, :].rearrange("e q i -> q e i"))
+                picked = rows[0:2, 0, r:16:SCALE_ROWS, :].rearrange("e q i -> q e i")
+                queue.dma_start(first_i[r:P:32, :, m, :], picked)
         words0 = keep.tile([P, 2 * 2 * 2 * H], U8, align_bytes=64, name="words0", tag="words0")
         words0_i = words0[:].bitcast(I32).rearrange("p (e m b) -> p e m b", e=2, m=2)
         for e in range(2):
@@ -130,7 +132,8 @@ def tile_moe_res_glu_sigmoid_kernel(
             nc.sync.dma_start(later_i[:, 0, m], src[2, 0])
         for r in range(SCALE_ROWS):
             for m, src in ((1, s3_i), (0, s1_i)):
-                nc.sync.dma_start(rest_i[r:P:32, :, m, :], src[2:E, 0, r:16:SCALE_ROWS, :].rearrange("e q i -> q e i"))
+                picked = src[2:E, 0, r:16:SCALE_ROWS, :].rearrange("e q i -> q e i")
+                nc.sync.dma_start(rest_i[r:P:32, :, m, :], picked)
         nc.sync.dma_start(gates[:, C:], gate[0:P, C:])
         for m, src in ((1, w3_i), (0, w1_i)):
             nc.sync.dma_start(later_i[:, 1, m], src[3, 0])
@@ -144,10 +147,11 @@ def tile_moe_res_glu_sigmoid_kernel(
 
         def scatter(e, r):
             window = windows[r][:].indirect(entries(e * C, (e + 1) * C))
-            if e < E - 1:
-                nc.vector.tensor_copy(window, gated[e, r][:])
+            if e < GATED:
+                nc.vector.tensor_copy(window, y[:, e, r, :])
             else:
-                nc.vector.tensor_tensor(window, last[:], gates[:, e * C : (e + 1) * C], MULT)
+                values = y[:, e, r, :] if e < E - 1 else last[:]
+                nc.vector.tensor_tensor(window, values, gates[:, e * C : (e + 1) * C], MULT)
 
         head_codes = keep.tile([P, 2 * C], U32, align_bytes=64, name="head_codes")
         head_scales = keep.tile([P, 2 * C], U8, align_bytes=64, name="head_scales")
@@ -157,7 +161,7 @@ def tile_moe_res_glu_sigmoid_kernel(
         x_codes = [head_codes[:, 0:C], head_codes[:, C : 2 * C]]
         x_scales = [head_scales[:, 0:C], head_scales[:, C : 2 * C]]
 
-        late_gathers = ((scales, x_scales, U8, 2, 3), (codes, x_codes, U32, 3, 4), (scales, x_scales, U8, 3, 4))
+        late_gathers = ((scales, x_scales, U8, 2), (codes, x_codes, U32, 3), (scales, x_scales, U8, 3))
         third = keep.tile([P, C], U32, align_bytes=64, name="third")
         nc.vector.tensor_copy(third[:], codes[:].indirect(entries(2 * C, 3 * C)))
         x_codes.append(third[:])
@@ -171,7 +175,7 @@ def tile_moe_res_glu_sigmoid_kernel(
                 return "bank4", "y_bank1"
             return (f"y_bank{(k // 2 - 1) % 2}" if k > 0 and k % 2 == 0 else "bank4"), "bank5"
 
-        ready, hs, turned_h, y_banks, gated, extra = {}, {}, {}, {}, {}, {}
+        ready, hs, turned_h, y_banks, extra = {}, {}, {}, {}, {}
 
         def first_products(n):
             k, s = divmod(n, 2)
@@ -202,7 +206,7 @@ def tile_moe_res_glu_sigmoid_kernel(
                 plain = keep.tile([P, HALF], F32, align_bytes=64, name="plain", tag=f"plain{k % 3}")[:]
                 nc.scalar.copy(plain.rearrange("p (u w v) -> p u w v", u=2, v=2), pair[1])
                 ready[n] = (plain, sig)
-            elif k >= SHARED and k % 2 == 1:
+            elif k >= SHARED and k % 2 == 1 and k // 2 <= GATED:
                 more = keep.tile([P, HALF // 2], F32, align_bytes=64, name="more", tag="more")[:]
                 nc.scalar.copy(more.rearrange("p (w v) -> p w v", v=2), pair[1][:, 0])
                 extra[k] = (more, sig[:, 0 : HALF // 2])
@@ -215,26 +219,24 @@ def tile_moe_res_glu_sigmoid_kernel(
             if s == 0 and k >= SHARED:
                 h = keep.tile([P, HALF + HALF // 2], BF16, align_bytes=64, name="h0", tag=f"swap{k % 2}")
                 nc.gpsimd.tensor_tensor(h[:, 0:HALF], *ready[n], MULT)
-                quarters = [h[:, 0 : HALF // 2], h[:, HALF // 2 : HALF]]
+                halves = [h[:, 0 : HALF // 2], h[:, HALF // 2 : HALF]]
                 if k in extra:
                     nc.gpsimd.tensor_tensor(h[:, HALF:], *extra[k], MULT)
-                    quarters.append(h[:, HALF:])
+                    halves.append(h[:, HALF:])
             elif s == 1 and k in extra:
                 h = ring.tile([P, HALF // 2], BF16, align_bytes=64, name="h1")
                 nc.vector.tensor_tensor(h[:].rearrange("p (w v) -> p w v", v=2), *ready[n], MULT)
-                quarters = [h[:]]
+                halves = [h[:]]
             else:
                 h = ring.tile([P, HALF], BF16, align_bytes=64, name="h1")
                 nc.vector.tensor_tensor(h[:].rearrange("p (u w v) -> p u w v", u=2, v=2), *ready[n], MULT)
-                quarters = [h[:, 0 : HALF // 2], h[:, HALF // 2 : HALF]]
-            hs[n] = quarters
+                halves = [h[:, 0 : HALF // 2], h[:, HALF // 2 : HALF]]
+            hs[n] = halves
 
         def turn(k):
-            tag = f"bank{(k + 1) % 2}"
-            turned = psum.tile([P, 2, 2, P], F32, name="turned", tag=tag)
-            for s in range(2):
-                for u in range(2):
-                    nc.tensor.transpose(turned[:, s, u, :], (hs[2 * k] + hs[2 * k + 1])[2 * s + u].bitcast(F32), ident[:])
+            turned = psum.tile([P, 2, 2, P], F32, name="turned", tag=f"bank{(k + 1) % 2}")
+            for b, part in enumerate(hs[2 * k] + hs[2 * k + 1]):
+                nc.tensor.transpose(turned[:, b // 2, b % 2, :], part.bitcast(F32), ident[:])
             if k + 1 >= LAG:
                 low = windows[(k + 1 - LAG) % 2][:, T : T + 2 * P]
             else:
@@ -249,7 +251,9 @@ def tile_moe_res_glu_sigmoid_kernel(
             h_scales = ring.tile([P, 2 * P], U8, align_bytes=64, name="h_scales")
             for s, half in enumerate(turned_h[k]):
                 cols = slice(s * P, (s + 1) * P)
-                nc.vector.quantize_mx(out=h_codes[:, cols].bitcast(FP8X4), scales=h_scales[:, cols], in_=half.bitcast(BF16))
+                nc.vector.quantize_mx(
+                    out=h_codes[:, cols].bitcast(FP8X4), scales=h_scales[:, cols], in_=half.bitcast(BF16)
+                )
             return h_codes, h_scales
 
         def second_product(k, h_codes, h_scales):
@@ -281,19 +285,21 @@ def tile_moe_res_glu_sigmoid_kernel(
             if k > 0:
                 second_product(k - 1, *quantised)
             product(2 * k + 1)
-            if k >= 2 and k % 2 == 0:
+            if k > 0 and k % 2 == 0:
                 e = k // 2 - 1
-                both = gates[:, e * C : (e + 1) * C].unsqueeze(1).to_broadcast([P, N // P, C])
-                nc.vector.tensor_tensor(y[:, e], y_banks[e][:], both, MULT)
-                gated[e, 0], gated[e, 1] = y[:, e, 0, :], y[:, e, 1, :]
+                if e < GATED:
+                    both = gates[:, e * C : (e + 1) * C].unsqueeze(1).to_broadcast([P, N // P, C])
+                    nc.vector.tensor_tensor(y[:, e], y_banks[e][:], both, MULT)
+                else:
+                    nc.scalar.copy(y[:, e], y_banks[e][:])
             if k >= LAG:
                 scatter(*divmod(k - LAG, 2))
             turn(k)
             if k < LAG:
-                table, kept, dtype, a, b = late_gathers[k]
-                late = keep.tile([P, (b - a) * C], dtype, align_bytes=64, name="late", tag=f"late{k}")
-                nc.vector.tensor_copy(late[:], table[:].indirect(entries(a * C, b * C)))
-                kept.extend(late[:, c * C : (c + 1) * C] for c in range(b - a))
+                table, kept, dtype, e = late_gathers[k]
+                late = keep.tile([P, C], dtype, align_bytes=64, name="late", tag=f"late{k}")
+                nc.vector.tensor_copy(late[:], table[:].indirect(entries(e * C, (e + 1) * C)))
+                kept.append(late[:])
             for n in (2 * k + AHEAD, 2 * k + AHEAD + 1):
                 if n < steps:
                     first_products(n)

@@ -171,7 +171,7 @@ def tile_moe_res_glu_sigmoid_kernel(
         def bank_tags(k, s):
             if s == 1:
                 return f"bank{k % 2}", f"bank{2 + k % 2}"
-            if k == 1:
+            if k in (1, 3):
                 return "bank4", "y_bank1"
             return (f"y_bank{(k // 2 - 1) % 2}" if k > 0 and k % 2 == 0 else "bank4"), "bank5"
 
@@ -237,10 +237,14 @@ def tile_moe_res_glu_sigmoid_kernel(
             turned = psum.tile([P, 2, 2, P], F32, name="turned", tag=f"bank{(k + 1) % 2}")
             for b, part in enumerate(hs[2 * k] + hs[2 * k + 1]):
                 nc.tensor.transpose(turned[:, b // 2, b % 2, :], part.bitcast(F32), ident[:])
-            if k + 1 >= LAG:
-                low = windows[(k + 1 - LAG) % 2][:, T : T + 2 * P]
-            else:
-                low = ring.tile([P, 2 * P], F32, align_bytes=64, name="low")[:]
+            if k + 1 < LAG:
+                whole = keep.tile([P, 4 * P], F32, align_bytes=64, name="whole", tag=f"swap{k % 2}")[:]
+                nc.scalar.copy(
+                    whole.rearrange("p (s c u) -> p s c u", s=2, u=2), turned[:].rearrange("p s u c -> p s c u")
+                )
+                turned_h[k] = (whole,)
+                return
+            low = windows[(k + 1 - LAG) % 2][:, T : T + 2 * P]
             high = keep.tile([P, 2 * P], F32, align_bytes=64, name="high", tag=f"swap{k % 2}")[:]
             for s, half in enumerate((low, high)):
                 nc.scalar.copy(half.rearrange("p (c u) -> p c u", u=2), turned[:, s].rearrange("p u c -> p c u"))
@@ -249,8 +253,9 @@ def tile_moe_res_glu_sigmoid_kernel(
         def quantise(k):
             h_codes = ring.tile([P, 2 * P], U32, align_bytes=64, name="h_codes")
             h_scales = ring.tile([P, 2 * P], U8, align_bytes=64, name="h_scales")
+            width = 2 * P // len(turned_h[k])
             for s, half in enumerate(turned_h[k]):
-                cols = slice(s * P, (s + 1) * P)
+                cols = slice(s * width, (s + 1) * width)
                 nc.vector.quantize_mx(
                     out=h_codes[:, cols].bitcast(FP8X4), scales=h_scales[:, cols], in_=half.bitcast(BF16)
                 )

@@ -15,6 +15,7 @@ U8 = mybir.dt.uint8
 FP8X4 = mybir.dt.float8_e4m3fn_x4
 FP4X4 = mybir.dt.float4_e2m1fn_x4
 SIGMOID = mybir.ActivationFunctionType.Sigmoid
+COPY = mybir.ActivationFunctionType.Copy
 MULT = mybir.AluOpType.mult
 ADD = mybir.AluOpType.add
 
@@ -26,12 +27,9 @@ CAST = 256
 SCALAR_EIGHTHS = 3
 HALF = 512
 FIRST = 160
-LAG = 3
-SHARED = 3
-GATED = 2
-AHEAD = 4
-TURNED = 4
-PIECES = ((0, TURNED * P, T), (1, 0, 384), (1, 384, 768), (1, 768, 1024), (1, 1024, T))
+SPARE = 512
+AHEAD = 3
+PIECES = ((0, 0, 640), (0, 640, T), (1, 0, 512), (1, 512, 1024), (1, 1024, T))
 
 
 def tile_moe_res_glu_sigmoid_kernel(
@@ -67,7 +65,7 @@ def tile_moe_res_glu_sigmoid_kernel(
         planes2_i = planes2_i.rearrange("p (e s n) -> p e s n", e=E, s=2)
         windows = []
         for r in range(N // P):
-            window = keep.tile([P, T + 2 * P], F32, align_bytes=64, name=f"window{r}")
+            window = keep.tile([P, T + SPARE], F32, align_bytes=64, name=f"window{r}")
             nc.scalar.copy(window[:, 0:T], zeros[r][:].to_broadcast([P, T]))
             windows.append(window)
         ident = keep.tile([P, P], F32, name="ident")
@@ -139,19 +137,8 @@ def tile_moe_res_glu_sigmoid_kernel(
             nc.sync.dma_start(later_i[:, 1, m], src[3, 0])
         nc.sync.dma_start(words2_i[:, E:, :], w2_i[2:E].rearrange("e s p b -> p (e s) b"))
 
-        y = keep.tile([P, E - 1, N // P, C], F32, name="y")
-        last = keep.tile([P, C], F32, name="last")
-
         def entries(a, b):
             return offsets[:, a // 16 : b // 16]
-
-        def scatter(e, r):
-            window = windows[r][:].indirect(entries(e * C, (e + 1) * C))
-            if e < GATED:
-                nc.vector.tensor_copy(window, y[:, e, r, :])
-            else:
-                values = y[:, e, r, :] if e < E - 1 else last[:]
-                nc.vector.tensor_tensor(window, values, gates[:, e * C : (e + 1) * C], MULT)
 
         head_codes = keep.tile([P, 2 * C], U32, align_bytes=64, name="head_codes")
         head_scales = keep.tile([P, 2 * C], U8, align_bytes=64, name="head_scales")
@@ -160,22 +147,14 @@ def tile_moe_res_glu_sigmoid_kernel(
             nc.vector.tensor_copy(head_scales[:, a:b], scales[:].indirect(entries(a, b)))
         x_codes = [head_codes[:, 0:C], head_codes[:, C : 2 * C]]
         x_scales = [head_scales[:, 0:C], head_scales[:, C : 2 * C]]
-
-        late_gathers = ((scales, x_scales, U8, 2), (codes, x_codes, U32, 3), (scales, x_scales, U8, 3))
-        third = keep.tile([P, C], U32, align_bytes=64, name="third")
-        nc.vector.tensor_copy(third[:], codes[:].indirect(entries(2 * C, 3 * C)))
-        x_codes.append(third[:])
+        for table, kept, dtype in ((codes, x_codes, U32), (scales, x_scales, U8)):
+            third = keep.tile([P, C], dtype, align_bytes=64, name="third", tag=f"third{len(kept)}{dtype == U8}")
+            nc.vector.tensor_copy(third[:], table[:].indirect(entries(2 * C, 3 * C)))
+            kept.append(third[:])
+        late_gathers = {3: (codes, x_codes, U32), 5: (scales, x_scales, U8)}
         blocks = E * C // P
         steps = blocks * H // HALF
-
-        def bank_tags(k, s):
-            if s == 1:
-                return f"bank{k % 2}", f"bank{2 + k % 2}"
-            if k in (1, 3):
-                return "bank4", "y_bank1"
-            return (f"y_bank{(k // 2 - 1) % 2}" if k > 0 and k % 2 == 0 else "bank4"), "bank5"
-
-        ready, hs, turned_h, y_banks, extra = {}, {}, {}, {}, {}
+        ready, hs, y_banks = {}, {}, {}
 
         def first_products(n):
             k, s = divmod(n, 2)
@@ -184,7 +163,7 @@ def tile_moe_res_glu_sigmoid_kernel(
             i_cols = slice(s * HALF, (s + 1) * HALF)
             pair = []
             for m in range(2):
-                bank = psum.tile([P, HALF], F32, name="bank", tag=bank_tags(k, s)[m])
+                bank = psum.tile([P, HALF], F32, name="bank", tag=f"sums{m}{n % 3}")
                 pair.append(bank[:].rearrange("p (w u v) -> p u w v", u=2, v=2))
                 table = words0 if e < 2 else later
                 at = 2 * ((2 * (e % 2) + m) * H + s * HALF)
@@ -198,147 +177,106 @@ def tile_moe_res_glu_sigmoid_kernel(
                     start=True,
                     stop=True,
                 )
-            tag = f"late{k}" if k < LAG and s == 0 else f"{('even', 'odd')[s]}{k % 2}"
-            sig = keep.tile([P, HALF], F32, align_bytes=64, name="sig", tag=tag)[:]
+            if n == steps - 3:
+                sig = windows[0][:, T : T + HALF]
+            else:
+                tag = f"late{n}" if n in late_gathers else f"sig{n % 3}"
+                sig = keep.tile([P, HALF], F32, align_bytes=64, name="sig", tag=tag)[:]
             sig_v = sig.rearrange("p (u w v) -> p u w v", u=2, v=2)
             nc.scalar.activation(sig_v, pair[0], SIGMOID)
-            if s == 0 and k >= SHARED:
-                plain = keep.tile([P, HALF], F32, align_bytes=64, name="plain", tag=f"plain{k % 3}")[:]
-                nc.scalar.copy(plain.rearrange("p (u w v) -> p u w v", u=2, v=2), pair[1])
-                ready[n] = (plain, sig)
-            elif k >= SHARED and k % 2 == 1 and k // 2 <= GATED:
-                more = keep.tile([P, HALF // 2], F32, align_bytes=64, name="more", tag="more")[:]
-                nc.scalar.copy(more.rearrange("p (w v) -> p w v", v=2), pair[1][:, 0])
-                extra[k] = (more, sig[:, 0 : HALF // 2])
-                ready[n] = (pair[1][:, 1], sig_v[:, 1])
-            else:
-                ready[n] = (pair[1], sig_v)
+            ready[n] = (pair[1], sig_v)
 
         def product(n):
-            k, s = divmod(n, 2)
-            if s == 0 and k >= SHARED:
-                h = keep.tile([P, HALF + HALF // 2], BF16, align_bytes=64, name="h0", tag=f"swap{k % 2}")
-                nc.gpsimd.tensor_tensor(h[:, 0:HALF], *ready[n], MULT)
-                halves = [h[:, 0 : HALF // 2], h[:, HALF // 2 : HALF]]
-                if k in extra:
-                    nc.gpsimd.tensor_tensor(h[:, HALF:], *extra[k], MULT)
-                    halves.append(h[:, HALF:])
-            elif s == 1 and k in extra:
-                h = ring.tile([P, HALF // 2], BF16, align_bytes=64, name="h1")
-                nc.vector.tensor_tensor(h[:].rearrange("p (w v) -> p w v", v=2), *ready[n], MULT)
-                halves = [h[:]]
+            if n == steps - 1:
+                h = windows[1][:, T : T + HALF // 2].bitcast(BF16)
             else:
-                h = ring.tile([P, HALF], BF16, align_bytes=64, name="h1")
-                nc.vector.tensor_tensor(h[:].rearrange("p (u w v) -> p u w v", u=2, v=2), *ready[n], MULT)
-                halves = [h[:, 0 : HALF // 2], h[:, HALF // 2 : HALF]]
-            hs[n] = halves
+                h = ring.tile([P, HALF], BF16, align_bytes=64, name="h")[:]
+            nc.vector.tensor_tensor(h.rearrange("p (u w v) -> p u w v", u=2, v=2), *ready[n], MULT)
+            hs[n] = [h[:, 0 : HALF // 2], h[:, HALF // 2 : HALF]]
+            if n in late_gathers:
+                table, kept, dtype = late_gathers[n]
+                late = keep.tile([P, C], dtype, align_bytes=64, name="late", tag=f"late{n}")
+                nc.vector.tensor_copy(late[:], table[:].indirect(entries(3 * C, 4 * C)))
+                kept.append(late[:])
+
+        ys = keep.tile([P, N // P, E * C], F32, name="ys")
+        turned_h, quantised = {}, {}
 
         def turn(k):
-            turned = psum.tile([P, 2, 2, P], F32, name="turned", tag=f"bank{(k + 1) % 2}")
+            e, q = divmod(k, C // P)
+            turned = psum.tile([P, 2, 2, P], F32, name="turned", tag=f"turned{k % 2}")
             for b, part in enumerate(hs[2 * k] + hs[2 * k + 1]):
                 nc.tensor.transpose(turned[:, b // 2, b % 2, :], part.bitcast(F32), ident[:])
-            if k + 1 < LAG:
-                whole = keep.tile([P, 4 * P], F32, align_bytes=64, name="whole", tag=f"swap{k % 2}")[:]
-                nc.scalar.copy(
-                    whole.rearrange("p (s c u) -> p s c u", s=2, u=2), turned[:].rearrange("p s u c -> p s c u")
-                )
-                turned_h[k] = (whole,)
-                return
-            low = windows[(k + 1 - LAG) % 2][:, T : T + 2 * P]
-            high = keep.tile([P, 2 * P], F32, align_bytes=64, name="high", tag=f"swap{k % 2}")[:]
-            for s, half in enumerate((low, high)):
-                nc.scalar.copy(half.rearrange("p (c u) -> p c u", u=2), turned[:, s].rearrange("p u c -> p c u"))
-            turned_h[k] = (low, high)
-
-        def quantise(k):
-            h_codes = ring.tile([P, 2 * P], U32, align_bytes=64, name="h_codes")
-            h_scales = ring.tile([P, 2 * P], U8, align_bytes=64, name="h_scales")
-            width = 2 * P // len(turned_h[k])
-            for s, half in enumerate(turned_h[k]):
-                cols = slice(s * width, (s + 1) * width)
-                nc.vector.quantize_mx(
-                    out=h_codes[:, cols].bitcast(FP8X4), scales=h_scales[:, cols], in_=half.bitcast(BF16)
-                )
-            return h_codes, h_scales
-
-        def second_product(k, h_codes, h_scales):
-            e, q = divmod(k, C // P)
             if q == 0:
-                y_banks[e] = psum.tile([P, N // P, C], F32, name="y_bank", tag=f"y_bank{e % 2}")
-            for r in range(N // P):
+                turned_h[e] = ring.tile([P, 2 * 2 * C], F32, align_bytes=64, name="whole")[:]
+            place = turned_h[e].rearrange("p (s c u) -> p s c u", s=2, u=2)[:, :, q * P : (q + 1) * P, :]
+            nc.scalar.copy(place, turned[:].rearrange("p s u c -> p s c u"))
+
+        def quantise(e):
+            h_codes = ring.tile([P, 2 * C], U32, align_bytes=64, name="h_codes")
+            h_scales = ring.tile([P, 2 * C], U8, align_bytes=64, name="h_scales")
+            nc.vector.quantize_mx(out=h_codes[:].bitcast(FP8X4), scales=h_scales[:], in_=turned_h[e].bitcast(BF16))
+            quantised[e] = (h_codes, h_scales)
+
+        def second_product(e, rows, tag):
+            h_codes, h_scales = quantised[e]
+            y_bank = psum.tile([P, len(rows), C], F32, name="y_bank", tag=tag)
+            for j, r in enumerate(rows):
                 for s in range(2):
                     at = 2 * ((2 * e + s) * N + r * P)
                     nc.tensor.matmul_mx(
-                        out=y_banks[e][:, r, q * P : (q + 1) * P],
+                        out=y_bank[:, j, :],
                         lhsT=words2[:, at : at + 2 * P].bitcast(FP4X4),
                         lhsT_scale=planes2[:, e, s, r * P : (r + 1) * P],
-                        rhs=h_codes[:, s * P : (s + 1) * P].bitcast(FP8X4),
-                        rhs_scale=h_scales[:, s * P : (s + 1) * P],
+                        rhs=h_codes[:, s * C : (s + 1) * C].bitcast(FP8X4),
+                        rhs_scale=h_scales[:, s * C : (s + 1) * C],
                         start=(s == 0),
                         stop=(s == 1),
                     )
+            return y_bank
+
+        def gated(e, rows, y_bank):
+            slots = slice(e * C, (e + 1) * C)
+            both = gates[:, slots].unsqueeze(1).to_broadcast([P, len(rows), C])
+            nc.vector.tensor_tensor(ys[:, rows[0] : rows[-1] + 1, slots], y_bank[:], both, MULT)
+
+        def scatter(copy, r, a, b):
+            copy(windows[r][:].indirect(entries(a, b)), ys[:, r, a:b])
+
+        def scalar_copy(to, values):
+            nc.scalar.activation(to, values, COPY)
 
         for n in range(AHEAD):
             first_products(n)
         for k in range(blocks):
-            if k < SHARED:
-                product(2 * k)
-            if k > 0:
-                quantised = quantise(k - 1)
-            if SHARED <= k + 1 < blocks:
-                product(2 * k + 2)
-            if k > 0:
-                second_product(k - 1, *quantised)
+            product(2 * k)
             product(2 * k + 1)
-            if k > 0 and k % 2 == 0:
-                e = k // 2 - 1
-                if e < GATED:
-                    both = gates[:, e * C : (e + 1) * C].unsqueeze(1).to_broadcast([P, N // P, C])
-                    nc.vector.tensor_tensor(y[:, e], y_banks[e][:], both, MULT)
-                else:
-                    nc.scalar.copy(y[:, e], y_banks[e][:])
-            if k >= LAG:
-                scatter(*divmod(k - LAG, 2))
             turn(k)
-            if k < LAG:
-                table, kept, dtype, e = late_gathers[k]
-                late = keep.tile([P, C], dtype, align_bytes=64, name="late", tag=f"late{k}")
-                nc.vector.tensor_copy(late[:], table[:].indirect(entries(e * C, (e + 1) * C)))
-                kept.append(late[:])
+            if k % 2 == 1 and k < blocks - 1:
+                quantise(k // 2)
+            if k == 1:
+                gated(0, (0, 1), second_product(0, (0, 1), "turned1"))
             for n in (2 * k + AHEAD, 2 * k + AHEAD + 1):
                 if n < steps:
                     first_products(n)
-        second_product(blocks - 1, *quantise(blocks - 1))
+            if k == blocks - 2:
+                gated(1, (0, 1), second_product(1, (0, 1), "sums01"))
+        gated(2, (1,), second_product(2, (1,), "sums02"))
+        scatter(scalar_copy, 0, 0, C)
+        scatter(nc.vector.tensor_copy, 0, C, 2 * C)
+        quantise(E - 1)
+        gated(2, (0,), second_product(2, (0,), "turned1"))
+        last_bank = second_product(3, (0, 1), "sums11")
+        scatter(scalar_copy, 1, 0, 384)
+        scatter(nc.vector.tensor_copy, 0, 2 * C, 3 * C)
+        scatter(scalar_copy, 1, 384, 3 * C)
+        gated(3, (0, 1), last_bank)
+        scatter(nc.vector.tensor_copy, 0, 3 * C, 4 * C)
+        scatter(scalar_copy, 1, 3 * C, 4 * C)
 
         residual = keep.tile([P, N // P, T], F32, align_bytes=64, name="residual", tag="words0")
         nc.sync.dma_start(residual[:], xr.rearrange("(r p) t -> p r t", p=P))
-        nc.scalar.copy(last[:], y_banks[E - 1][:, 0, :])
-        scatter(E - 2, 1)
-
-        sums = []
-        for b in range(TURNED):
-            bank = psum.tile([P, P], F32, name="sum_bank", tag=f"bank{b}")
-            nc.tensor.matmul(
-                bank[:], residual[:, 0, b * P : (b + 1) * P], ident[:], start=True, stop=False, is_transpose=True
-            )
-            sums.append(bank)
-        scatter(E - 1, 0)
-        nc.scalar.copy(last[:], y_banks[E - 1][:, 1, :])
-        across = keep.tile([P, TURNED, P], F32, name="across")
-        for b, bank in enumerate(sums):
-            nc.tensor.matmul(
-                bank[:], windows[0][:, b * P : (b + 1) * P], ident[:], start=False, stop=True, is_transpose=True
-            )
-            nc.scalar.copy(across[:, b, :], bank[:])
-        back = psum.tile([P, TURNED, P], F32, name="back", tag="bank4")
-        for b in range(TURNED):
-            nc.tensor.transpose(back[:, b, :], across[:, b, :], ident[:])
-        done = keep.tile([P, TURNED * P], F32, name="done")
-        nc.scalar.copy(done[:], back[:].rearrange("p b c -> p (b c)"))
-        nc.scalar.dma_start(out[0:P, 0 : TURNED * P], done[:])
         for r, a, b in PIECES:
-            if (r, a) == (1, 0):
-                scatter(E - 1, 1)
             total = keep.tile([P, b - a], F32, name=f"total{r}{a}")
             nc.vector.tensor_tensor(total[:], windows[r][:, a:b], residual[:, r, a:b], ADD)
             nc.sync.dma_start(out[r * P : (r + 1) * P, a:b], total[:])

@@ -59,15 +59,11 @@ def tile_moe_res_glu_sigmoid_kernel(
         rest_i = rest[:].rearrange("p e m i -> p (e m i)").bitcast(I32)
         nc.vector.memset(rest_i, 0)
         rest_i = rest_i.rearrange("p (e m i) -> p e m i", e=2, m=2)
-        planes2 = keep.tile([P, E, 2, N], U8, align_bytes=64, name="planes2")
-        planes2_i = planes2[:].rearrange("p e s n -> p (e s n)").bitcast(I32)
-        nc.vector.memset(planes2_i, 0)
-        planes2_i = planes2_i.rearrange("p (e s n) -> p e s n", e=E, s=2)
         windows = []
         for r in range(N // P):
             window = keep.tile([P, T + SPARE], F32, align_bytes=64, name=f"window{r}")
-            nc.scalar.copy(window[:, 0:T], zeros[r][:].to_broadcast([P, T]))
             windows.append(window)
+        nc.scalar.copy(windows[0][:, 0:T], zeros[0][:].to_broadcast([P, T]))
         ident = keep.tile([P, P], F32, name="ident")
         make_identity(nc, ident[:])
 
@@ -87,15 +83,17 @@ def tile_moe_res_glu_sigmoid_kernel(
             nc.sync.dma_start(raw, x_rows[:, :, t0 : t0 + width])
             raws.append((t0, width, raw))
             t0 += width
-        for m, (queue, rows) in enumerate(((nc.sync, s1_i), (nc.gpsimd, s3_i))):
+        words0 = keep.tile([P, 2 * 2 * 2 * H], U8, align_bytes=64, name="words0", tag="words0")
+        words0_i = words0[:].bitcast(I32).rearrange("p (e m b) -> p e m b", e=2, m=2)
+        for m, src in enumerate((w1_i, w3_i)):
+            nc.sync.dma_start(words0_i[:, 0, m, :], src[0, 0])
+        for m, (queue, rows) in enumerate(((nc.sync, s1_i), (nc.scalar, s3_i))):
             for r in range(SCALE_ROWS):
                 picked = rows[0:2, 0, r:16:SCALE_ROWS, :].rearrange("e q i -> q e i")
                 queue.dma_start(first_i[r:P:32, :, m, :], picked)
-        words0 = keep.tile([P, 2 * 2 * 2 * H], U8, align_bytes=64, name="words0", tag="words0")
-        words0_i = words0[:].bitcast(I32).rearrange("p (e m b) -> p e m b", e=2, m=2)
-        for e in range(2):
-            for m, src in enumerate((w1_i, w3_i)):
-                nc.sync.dma_start(words0_i[:, e, m, :], src[e, 0])
+        for m, src in enumerate((w1_i, w3_i)):
+            nc.sync.dma_start(words0_i[:, 1, m, :], src[1, 0])
+        nc.scalar.copy(windows[1][:, 0:T], zeros[1][:].to_broadcast([P, T]))
 
         grouped = keep.tile([P, T, PACK], BF16, align_bytes=64, name="grouped", tag="grouped")
         for t0, width, raw in raws:
@@ -114,11 +112,25 @@ def tile_moe_res_glu_sigmoid_kernel(
                     in_=grouped[:, cols, :].rearrange("p t j -> p (t j)"),
                 )
 
-        later = keep.tile([P, 2 * (E - 2) * 2 * H], U8, align_bytes=64, name="later", tag="stage1")
+        planes2 = keep.tile([P, E, 2, N], U8, align_bytes=64, name="planes2", tag="stage1")
+        planes2_i = planes2[:].rearrange("p e s n -> p (e s n)").bitcast(I32)
+        nc.scalar.copy(
+            planes2_i.bitcast(U32).rearrange("p (e i) -> p e i", e=2), rest_i[:, :, 1, :].bitcast(U32)
+        )
+        planes2_i = planes2_i.rearrange("p (e s n) -> p e s n", e=E, s=2)
+        later = keep.tile([P, 2 * (E - 2) * 2 * H], U8, align_bytes=64, name="later", tag="stage0")
         later_i = later[:].bitcast(I32).rearrange("p (e m b) -> p e m b", m=2, e=E - 2)
-        words2 = keep.tile([P, E * 2 * 2 * N], U8, align_bytes=64, name="words2", tag="stage0")
+        words2 = keep.tile([P, E * 2 * 2 * N], U8, align_bytes=64, name="words2")
         words2_i = words2[:].bitcast(I32).rearrange("p (x b) -> p x b", b=N // 2)
         gates = keep.tile([P, E * C], F32, align_bytes=64, name="gates", tag="grouped")[:]
+        for m, src in ((1, w3_i), (0, w1_i)):
+            nc.sync.dma_start(later_i[:, 0, m], src[2, 0])
+        for r in range(SCALE_ROWS):
+            for m, (queue, src) in enumerate(((nc.sync, s1_i), (nc.scalar, s3_i))):
+                picked = src[2:E, 0, r:16:SCALE_ROWS, :].rearrange("e q i -> q e i")
+                queue.dma_start(rest_i[r:P:32, :, m, :], picked)
+        for m, src in ((1, w3_i), (0, w1_i)):
+            nc.sync.dma_start(later_i[:, 1, m], src[3, 0])
         for r in range(SCALE_ROWS):
             nc.sync.dma_start(
                 planes2_i[r:P:32].rearrange("q e s n -> q (e s) n"),
@@ -126,15 +138,7 @@ def tile_moe_res_glu_sigmoid_kernel(
             )
         nc.sync.dma_start(words2_i[:, 0:E, :], w2_i[0:2].rearrange("e s p b -> p (e s) b"))
         nc.sync.dma_start(gates[:, 0:C], gate[0:P, 0:C])
-        for m, src in ((1, w3_i), (0, w1_i)):
-            nc.sync.dma_start(later_i[:, 0, m], src[2, 0])
-        for r in range(SCALE_ROWS):
-            for m, src in ((1, s3_i), (0, s1_i)):
-                picked = src[2:E, 0, r:16:SCALE_ROWS, :].rearrange("e q i -> q e i")
-                nc.sync.dma_start(rest_i[r:P:32, :, m, :], picked)
         nc.sync.dma_start(gates[:, C:], gate[0:P, C:])
-        for m, src in ((1, w3_i), (0, w1_i)):
-            nc.sync.dma_start(later_i[:, 1, m], src[3, 0])
         nc.sync.dma_start(words2_i[:, E:, :], w2_i[2:E].rearrange("e s p b -> p (e s) b"))
 
         def entries(a, b):
@@ -233,12 +237,12 @@ def tile_moe_res_glu_sigmoid_kernel(
                         start=(s == 0),
                         stop=(s == 1),
                     )
-            return y_bank
+            return y_bank[:]
 
         def gated(e, rows, y_bank):
             slots = slice(e * C, (e + 1) * C)
             both = gates[:, slots].unsqueeze(1).to_broadcast([P, len(rows), C])
-            nc.vector.tensor_tensor(ys[:, rows[0] : rows[-1] + 1, slots], y_bank[:], both, MULT)
+            nc.vector.tensor_tensor(ys[:, rows[0] : rows[-1] + 1, slots], y_bank, both, MULT)
 
         def scatter(copy, r, a, b):
             copy(windows[r][:].indirect(entries(a, b)), ys[:, r, a:b])
@@ -254,8 +258,8 @@ def tile_moe_res_glu_sigmoid_kernel(
             turn(k)
             if k % 2 == 1 and k < blocks - 1:
                 quantise(k // 2)
-            if k == 1:
-                gated(0, (0, 1), second_product(0, (0, 1), "turned1"))
+            if k == 4:
+                gated(0, (0, 1), second_product(0, (0, 1), "turned0"))
             for n in (2 * k + AHEAD, 2 * k + AHEAD + 1):
                 if n < steps:
                     first_products(n)
@@ -270,7 +274,8 @@ def tile_moe_res_glu_sigmoid_kernel(
         scatter(scalar_copy, 1, 0, 384)
         scatter(nc.vector.tensor_copy, 0, 2 * C, 3 * C)
         scatter(scalar_copy, 1, 384, 3 * C)
-        gated(3, (0, 1), last_bank)
+        for r in range(N // P):
+            gated(3, (r,), last_bank[:, r : r + 1, :])
         scatter(nc.vector.tensor_copy, 0, 3 * C, 4 * C)
         scatter(scalar_copy, 1, 3 * C, 4 * C)
 

@@ -29,7 +29,8 @@ HALF = 512
 FIRST = 160
 SPARE = 512
 AHEAD = 3
-PIECES = ((0, 0, 640), (0, 640, T), (1, 0, 512), (1, 512, 1024), (1, 1024, T))
+TURNED = 2
+PIECES = ((0, 0, 512), (0, 512, T - TURNED * P), (1, 0, 512), (1, 512, 1024), (1, 1024, T))
 
 
 def tile_moe_res_glu_sigmoid_kernel(
@@ -281,6 +282,20 @@ def tile_moe_res_glu_sigmoid_kernel(
 
         residual = keep.tile([P, N // P, T], F32, align_bytes=64, name="residual", tag="words0")
         nc.sync.dma_start(residual[:], xr.rearrange("(r p) t -> p r t", p=P))
+        cols = [slice(T - (TURNED - j) * P, T - (TURNED - j - 1) * P) for j in range(TURNED)]
+        sums = [psum.tile([P, P], F32, name="sums", tag=f"sums0{j}") for j in range(TURNED)]
+        for j in range(TURNED):
+            nc.tensor.matmul(sums[j][:], residual[:, 0, cols[j]], ident[:], start=True, stop=False, is_transpose=True)
+        for j in range(TURNED):
+            nc.tensor.matmul(sums[j][:], windows[0][:, cols[j]], ident[:], start=False, stop=True, is_transpose=True)
+        by_token = keep.tile([P, TURNED, P], F32, name="by_token")
+        back = psum.tile([P, TURNED, P], F32, name="back", tag="turned0")
+        for j in range(TURNED):
+            nc.scalar.copy(by_token[:, j, :], sums[j][:])
+            nc.tensor.transpose(back[:, j, :], by_token[:, j, :], ident[:])
+        ends = keep.tile([P, TURNED * P], F32, name="ends")
+        nc.scalar.copy(ends[:], back[:].rearrange("p j t -> p (j t)"))
+        nc.scalar.dma_start(out[0:P, T - TURNED * P : T], ends[:])
         for r, a, b in PIECES:
             total = keep.tile([P, b - a], F32, name=f"total{r}{a}")
             nc.vector.tensor_tensor(total[:], windows[r][:, a:b], residual[:, r, a:b], ADD)

@@ -27,6 +27,7 @@ CAST = 256
 SCALAR_EIGHTHS = 3
 HALF = 512
 FIRST = 160
+LENT = 160
 SPARE = 512
 AHEAD = 3
 TURNED = 2
@@ -62,7 +63,7 @@ def tile_moe_res_glu_sigmoid_kernel(
         rest_i = rest_i.rearrange("p (e m i) -> p e m i", e=2, m=2)
         windows = []
         for r in range(N // P):
-            window = keep.tile([P, T + SPARE], F32, align_bytes=64, name=f"window{r}")
+            window = keep.tile([P, T + r * SPARE], F32, align_bytes=64, name=f"window{r}")
             windows.append(window)
         nc.scalar.copy(windows[0][:, 0:T], zeros[0][:].to_broadcast([P, T]))
         ident = keep.tile([P, P], F32, name="ident")
@@ -182,11 +183,8 @@ def tile_moe_res_glu_sigmoid_kernel(
                     start=True,
                     stop=True,
                 )
-            if n == steps - 3:
-                sig = windows[0][:, T : T + HALF]
-            else:
-                tag = f"late{n}" if n in late_gathers else f"sig{n % 3}"
-                sig = keep.tile([P, HALF], F32, align_bytes=64, name="sig", tag=tag)[:]
+            tag = f"late{n}" if n in late_gathers else f"sig{n % 3}"
+            sig = keep.tile([P, HALF], F32, align_bytes=64, name="sig", tag=tag)[:]
             sig_v = sig.rearrange("p (u w v) -> p u w v", u=2, v=2)
             nc.scalar.activation(sig_v, pair[0], SIGMOID)
             ready[n] = (pair[1], sig_v)
@@ -267,8 +265,8 @@ def tile_moe_res_glu_sigmoid_kernel(
             if k == blocks - 2:
                 gated(1, (0, 1), second_product(1, (0, 1), "sums01"))
         gated(2, (1,), second_product(2, (1,), "sums02"))
-        scatter(scalar_copy, 0, 0, C)
-        scatter(nc.vector.tensor_copy, 0, C, 2 * C)
+        scatter(scalar_copy, 0, 0, LENT)
+        scatter(nc.vector.tensor_copy, 0, LENT, 2 * C)
         quantise(E - 1)
         gated(2, (0,), second_product(2, (0,), "turned1"))
         last_bank = second_product(3, (0, 1), "sums11")

from contextlib import ExitStack

import concourse.mybir as mybir
from concourse.masks import make_identity

K, T, E, C, H, N = 512, 1280, 4, 256, 1024, 256
FLOPS = 2 * E * C * (2 * K * H + H * N)

F32 = mybir.dt.float32
BF16 = mybir.dt.bfloat16
I32 = mybir.dt.int32
U32 = mybir.dt.uint32
U16 = mybir.dt.uint16
U8 = mybir.dt.uint8
FP8X4 = mybir.dt.float8_e4m3fn_x4
FP4X4 = mybir.dt.float4_e2m1fn_x4
SIGMOID = mybir.ActivationFunctionType.Sigmoid
COPY = mybir.ActivationFunctionType.Copy
MULT = mybir.AluOpType.mult
ADD = mybir.AluOpType.add

P = 128
PACK = 4
SCALE_ROWS = 4
LOADS = (512, 384, 256, 128)
CAST = 256
SCALAR_EIGHTHS = 3
HALF = 512
FIRST = 160
LENT = 160
SPARE = 512
AHEAD = 3
TURNED = 2
PIECES = ((0, 0, 512), (0, 512, T - TURNED * P), (1, 0, 512), (1, 512, 1024), (1, 1024, T))


def tile_moe_res_glu_sigmoid_kernel(
    tc, xT, xr, w1_words, w1_scales, w3_words, w3_scales, w2_words, w2_scales, gate, offs, out
):
    nc = tc.nc
    with ExitStack() as ctx:
        keep = ctx.enter_context(tc.tile_pool(name="keep", bufs=1))
        ring = ctx.enter_context(tc.tile_pool(name="ring", bufs=4))
        psum = ctx.enter_context(tc.psum_pool(name="psum", bufs=1))

        zeros = []
        for tag in ("words0", "zero"):
            zero = keep.tile([P, 1], F32, align_bytes=64, name="zero", tag=tag)
            nc.gpsimd.memset(zero[:], 0.0)
            zeros.append(zero)

        first = keep.tile([P, 2, 2, H], U8, align_bytes=64, name="first")
        first_i = first[:].rearrange("p e m i -> p (e m i)").bitcast(I32)
        for e, engine in enumerate((nc.vector, nc.gpsimd)):
            engine.memset(first_i[:, e * H // 2 : (e + 1) * H // 2], 0)
        first_i = first_i.rearrange("p (e m i) -> p e m i", e=2, m=2)
        codes = keep.tile([P, T], U32, align_bytes=64, name="codes")
        scales = keep.tile([P, T], U8, align_bytes=64, name="scales")
        nc.vector.memset(scales[:].bitcast(I32), 0)
        rest = keep.tile([P, 2, 2, H], U8, align_bytes=64, name="rest")
        rest_i = rest[:].rearrange("p e m i -> p (e m i)").bitcast(I32)
        nc.vector.memset(rest_i, 0)
        rest_i = rest_i.rearrange("p (e m i) -> p e m i", e=2, m=2)
        windows = []
        for r in range(N // P):
            window = keep.tile([P, T + r * SPARE], F32, align_bytes=64, name=f"window{r}")
            windows.append(window)
        nc.scalar.copy(windows[0][:, 0:T], zeros[0][:].to_broadcast([P, T]))
        ident = keep.tile([P, P], F32, name="ident")
        make_identity(nc, ident[:])

        s1_i, s3_i, s2_i = w1_scales.bitcast(I32), w3_scales.bitcast(I32), w2_scales.bitcast(I32)
        w1_i, w3_i, w2_i = w1_words.bitcast(I32), w3_words.bitcast(I32), w2_words.bitcast(I32)
        x_rows = xT.rearrange("(p j) t -> p j t", j=PACK)
        offsets = keep.tile([P, E * C // 16], U16, name="offsets")
        nc.sync.dma_start(offsets[:], offs)
        raw0 = keep.tile([P, PACK, LOADS[0]], F32, align_bytes=64, name="raw0", tag="stage0")
        nc.sync.dma_start(raw0[:], x_rows[:, :, 0 : LOADS[0]])
        raws = [(0, LOADS[0], raw0[:])]
        raw1 = keep.tile([P, PACK * (T - LOADS[0])], F32, align_bytes=64, name="raw1", tag="stage1")
        t0 = LOADS[0]
        for width in LOADS[1:]:
            at = PACK * (t0 - LOADS[0])
            raw = raw1[:, at : at + PACK * width].rearrange("p (j t) -> p j t", j=PACK)
            nc.sync.dma_start(raw, x_rows[:, :, t0 : t0 + width])
            raws.append((t0, width, raw))
            t0 += width
        words0 = keep.tile([P, 2 * 2 * 2 * H], U8, align_bytes=64, name="words0", tag="words0")
        words0_i = words0[:].bitcast(I32).rearrange("p (e m b) -> p e m b", e=2, m=2)
        for m, src in enumerate((w1_i, w3_i)):
            nc.sync.dma_start(words0_i[:, 0, m, :], src[0, 0])
        for m, (queue, rows) in enumerate(((nc.sync, s1_i), (nc.scalar, s3_i))):
            for r in range(SCALE_ROWS):
                picked = rows[0:2, 0, r:16:SCALE_ROWS, :].rearrange("e q i -> q e i")
                queue.dma_start(first_i[r:P:32, :, m, :], picked)
        for m, src in enumerate((w1_i, w3_i)):
            nc.sync.dma_start(words0_i[:, 1, m, :], src[1, 0])
        nc.scalar.copy(windows[1][:, 0:T], zeros[1][:].to_broadcast([P, T]))

        grouped = keep.tile([P, T, PACK], BF16, align_bytes=64, name="grouped", tag="grouped")
        for t0, width, raw in raws:
            for c in range(0, width, CAST):
                end = min(c + CAST, width)
                cut = c + SCALAR_EIGHTHS * (end - c) // 8
                for copy, a, b in ((nc.scalar.copy, c, cut), (nc.vector.tensor_copy, cut, end)):
                    copy(
                        grouped[:, t0 + a : t0 + b, :].rearrange("p (c i) j -> p c j i", i=4),
                        raw[:, :, a:b].rearrange("p j (c i) -> p c j i", i=4),
                    )
                cols = slice(t0 + c, t0 + end)
                nc.vector.quantize_mx(
                    out=codes[:, cols].bitcast(FP8X4),
                    scales=scales[:, cols],
                    in_=grouped[:, cols, :].rearrange("p t j -> p (t j)"),
                )

        planes2 = keep.tile([P, E, 2, N], U8, align_bytes=64, name="planes2", tag="stage1")
        planes2_i = planes2[:].rearrange("p e s n -> p (e s n)").bitcast(I32)
        nc.scalar.copy(
            planes2_i.bitcast(U32).rearrange("p (e i) -> p e i", e=2), rest_i[:, :, 1, :].bitcast(U32)
        )
        planes2_i = planes2_i.rearrange("p (e s n) -> p e s n", e=E, s=2)
        later = keep.tile([P, 2 * (E - 2) * 2 * H], U8, align_bytes=64, name="later", tag="stage0")
        later_i = later[:].bitcast(I32).rearrange("p (e m b) -> p e m b", m=2, e=E - 2)
        words2 = keep.tile([P, E * 2 * 2 * N], U8, align_bytes=64, name="words2")
        words2_i = words2[:].bitcast(I32).rearrange("p (x b) -> p x b", b=N // 2)
        gates = keep.tile([P, E * C], F32, align_bytes=64, name="gates", tag="grouped")[:]
        for m, src in ((1, w3_i), (0, w1_i)):
            nc.sync.dma_start(later_i[:, 0, m], src[2, 0])
        for r in range(SCALE_ROWS):
            for m, (queue, src) in enumerate(((nc.sync, s1_i), (nc.scalar, s3_i))):
                picked = src[2:E, 0, r:16:SCALE_ROWS, :].rearrange("e q i -> q e i")
                queue.dma_start(rest_i[r:P:32, :, m, :], picked)
        for m, src in ((1, w3_i), (0, w1_i)):
            nc.sync.dma_start(later_i[:, 1, m], src[3, 0])
        for r in range(SCALE_ROWS):
            nc.sync.dma_start(
                planes2_i[r:P:32].rearrange("q e s n -> q (e s) n"),
                s2_i[:, :, r:16:SCALE_ROWS, :].rearrange("e s q n -> q (e s) n"),
            )
        nc.sync.dma_start(words2_i[:, 0:E, :], w2_i[0:2].rearrange("e s p b -> p (e s) b"))
        nc.sync.dma_start(gates[:, 0:C], gate[0:P, 0:C])
        nc.sync.dma_start(gates[:, C:], gate[0:P, C:])
        nc.sync.dma_start(words2_i[:, E:, :], w2_i[2:E].rearrange("e s p b -> p (e s) b"))

        def entries(a, b):
            return offsets[:, a // 16 : b // 16]

        head_codes = keep.tile([P, 2 * C], U32, align_bytes=64, name="head_codes")
        head_scales = keep.tile([P, 2 * C], U8, align_bytes=64, name="head_scales")
        for a, b in ((0, FIRST), (FIRST, 2 * C)):
            nc.vector.tensor_copy(head_codes[:, a:b], codes[:].indirect(entries(a, b)))
            nc.vector.tensor_copy(head_scales[:, a:b], scales[:].indirect(entries(a, b)))
        x_codes = [head_codes[:, 0:C], head_codes[:, C : 2 * C]]
        x_scales = [head_scales[:, 0:C], head_scales[:, C : 2 * C]]
        for table, kept, dtype in ((codes, x_codes, U32), (scales, x_scales, U8)):
            third = keep.tile([P, C], dtype, align_bytes=64, name="third", tag=f"third{len(kept)}{dtype == U8}")
            nc.vector.tensor_copy(third[:], table[:].indirect(entries(2 * C, 3 * C)))
            kept.append(third[:])
        late_gathers = {3: (codes, x_codes, U32), 5: (scales, x_scales, U8)}
        blocks = E * C // P
        steps = blocks * H // HALF
        ready, hs, y_banks = {}, {}, {}

        def first_products(n):
            k, s = divmod(n, 2)
            e, q = divmod(k, C // P)
            slots = slice(q * P, (q + 1) * P)
            i_cols = slice(s * HALF, (s + 1) * HALF)
            pair = []
            for m in range(2):
                bank = psum.tile([P, HALF], F32, name="bank", tag=f"sums{m}{n % 3}")
                pair.append(bank[:].rearrange("p (w u v) -> p u w v", u=2, v=2))
                table = words0 if e < 2 else later
                at = 2 * ((2 * (e % 2) + m) * H + s * HALF)
                plane = (first, rest)[e // 2][:, e % 2, m, i_cols]
                nc.tensor.matmul_mx(
                    out=bank[:],
                    lhsT=x_codes[e][:, slots].bitcast(FP8X4),
                    lhsT_scale=x_scales[e][:, slots],
                    rhs=table[:, at : at + 2 * HALF].bitcast(FP4X4),
                    rhs_scale=plane,
                    start=True,
                    stop=True,
                )
            tag = f"late{n}" if n in late_gathers else f"sig{n % 3}"
            sig = keep.tile([P, HALF], F32, align_bytes=64, name="sig", tag=tag)[:]
            sig_v = sig.rearrange("p (u w v) -> p u w v", u=2, v=2)
            nc.scalar.activation(sig_v, pair[0], SIGMOID)
            ready[n] = (pair[1], sig_v)

        def product(n):
            if n == steps - 1:
                h = windows[1][:, T : T + HALF // 2].bitcast(BF16)
            else:
                h = ring.tile([P, HALF], BF16, align_bytes=64, name="h")[:]
            nc.vector.tensor_tensor(h.rearrange("p (u w v) -> p u w v", u=2, v=2), *ready[n], MULT)
            hs[n] = [h[:, 0 : HALF // 2], h[:, HALF // 2 : HALF]]
            if n in late_gathers:
                table, kept, dtype = late_gathers[n]
                late = keep.tile([P, C], dtype, align_bytes=64, name="late", tag=f"late{n}")
                nc.vector.tensor_copy(late[:], table[:].indirect(entries(3 * C, 4 * C)))
                kept.append(late[:])

        ys = keep.tile([P, N // P, E * C], F32, name="ys")
        turned_h, quantised = {}, {}

        def turn(k):
            e, q = divmod(k, C // P)
            turned = psum.tile([P, 2, 2, P], F32, name="turned", tag=f"turned{k % 2}")
            for b, part in enumerate(hs[2 * k] + hs[2 * k + 1]):
                nc.tensor.transpose(turned[:, b // 2, b % 2, :], part.bitcast(F32), ident[:])
            if q == 0:
                turned_h[e] = ring.tile([P, 2 * 2 * C], F32, align_bytes=64, name="whole")[:]
            place = turned_h[e].rearrange("p (s c u) -> p s c u", s=2, u=2)[:, :, q * P : (q + 1) * P, :]
            nc.scalar.copy(place, turned[:].rearrange("p s u c -> p s c u"))

        def quantise(e):
            h_codes = ring.tile([P, 2 * C], U32, align_bytes=64, name="h_codes")
            h_scales = ring.tile([P, 2 * C], U8, align_bytes=64, name="h_scales")
            nc.vector.quantize_mx(out=h_codes[:].bitcast(FP8X4), scales=h_scales[:], in_=turned_h[e].bitcast(BF16))
            quantised[e] = (h_codes, h_scales)

        def second_product(e, rows, tag):
            h_codes, h_scales = quantised[e]
            y_bank = psum.tile([P, len(rows), C], F32, name="y_bank", tag=tag)
            for j, r in enumerate(rows):
                for s in range(2):
                    at = 2 * ((2 * e + s) * N + r * P)
                    nc.tensor.matmul_mx(
                        out=y_bank[:, j, :],
                        lhsT=words2[:, at : at + 2 * P].bitcast(FP4X4),
                        lhsT_scale=planes2[:, e, s, r * P : (r + 1) * P],
                        rhs=h_codes[:, s * C : (s + 1) * C].bitcast(FP8X4),
                        rhs_scale=h_scales[:, s * C : (s + 1) * C],
                        start=(s == 0),
                        stop=(s == 1),
                    )
            return y_bank[:]

        def gated(e, rows, y_bank):
            slots = slice(e * C, (e + 1) * C)
            both = gates[:, slots].unsqueeze(1).to_broadcast([P, len(rows), C])
            nc.vector.tensor_tensor(ys[:, rows[0] : rows[-1] + 1, slots], y_bank, both, MULT)

        def scatter(copy, r, a, b):
            copy(windows[r][:].indirect(entries(a, b)), ys[:, r, a:b])

        def scalar_copy(to, values):
            nc.scalar.activation(to, values, COPY)

        for n in range(AHEAD):
            first_products(n)
        for k in range(blocks):
            product(2 * k)
            product(2 * k + 1)
            turn(k)
            if k % 2 == 1 and k < blocks - 1:
                quantise(k // 2)
            if k == 4:
                gated(0, (0, 1), second_product(0, (0, 1), "turned0"))
            for n in (2 * k + AHEAD, 2 * k + AHEAD + 1):
                if n < steps:
                    first_products(n)
            if k == blocks - 2:
                gated(1, (0, 1), second_product(1, (0, 1), "sums01"))
        gated(2, (1,), second_product(2, (1,), "sums02"))
        scatter(scalar_copy, 0, 0, LENT)
        scatter(nc.vector.tensor_copy, 0, LENT, 2 * C)
        quantise(E - 1)
        gated(2, (0,), second_product(2, (0,), "turned1"))
        last_bank = second_product(3, (0, 1), "sums11")
        scatter(scalar_copy, 1, 0, 384)
        scatter(nc.vector.tensor_copy, 0, 2 * C, 3 * C)
        scatter(scalar_copy, 1, 384, 3 * C)
        for r in range(N // P):
            gated(3, (r,), last_bank[:, r : r + 1, :])
        scatter(nc.vector.tensor_copy, 0, 3 * C, 4 * C)
        scatter(scalar_copy, 1, 3 * C, 4 * C)

        residual = keep.tile([P, N // P, T], F32, align_bytes=64, name="residual", tag="words0")
        nc.sync.dma_start(residual[:], xr.rearrange("(r p) t -> p r t", p=P))
        cols = [slice(T - (TURNED - j) * P, T - (TURNED - j - 1) * P) for j in range(TURNED)]
        sums = [psum.tile([P, P], F32, name="sums", tag=f"sums0{j}") for j in range(TURNED)]
        for j in range(TURNED):
            nc.tensor.matmul(sums[j][:], residual[:, 0, cols[j]], ident[:], start=True, stop=False, is_transpose=True)
        for j in range(TURNED):
            nc.tensor.matmul(sums[j][:], windows[0][:, cols[j]], ident[:], start=False, stop=True, is_transpose=True)
        by_token = keep.tile([P, TURNED, P], F32, name="by_token")
        back = psum.tile([P, TURNED, P], F32, name="back", tag="turned0")
        for j in range(TURNED):
            nc.scalar.copy(by_token[:, j, :], sums[j][:])
            nc.tensor.transpose(back[:, j, :], by_token[:, j, :], ident[:])
        ends = keep.tile([P, TURNED * P], F32, name="ends")
        nc.scalar.copy(ends[:], back[:].rearrange("p j t -> p (j t)"))
        nc.scalar.dma_start(out[0:P, T - TURNED * P : T], ends[:])
        for r, a, b in PIECES:
            total = keep.tile([P, b - a], F32, name=f"total{r}{a}")
            nc.vector.tensor_tensor(total[:], windows[r][:, a:b], residual[:, r, a:b], ADD)
            nc.sync.dma_start(out[r * P : (r + 1) * P, a:b], total[:])
